import numpy as np, ml_dtypes
CORES = [2,6,10,14,18,22,26,30]
N = 8
BF = ml_dtypes.bfloat16
def gentries(a):
    return np.ascontiguousarray(a.reshape(8, 16, -1).transpose(0, 2, 1)).reshape(8, -1)
def gtable(e):
    e = np.asarray(e); return np.ascontiguousarray(e.reshape(8, -1, 16).transpose(0, 2, 1)).reshape(128, -1).astype(np.int32)
V, P, T, TL, Q, M = 2560, 192, 4, 2, 8, 4096
def money(rng, base):
    v = base + rng.integers(-3, 4, base.shape[:2] + (16, base.shape[-1]))
    return np.clip(np.floor(v), 0, 15).astype(np.int64)
def parts(rng):
    x = money(rng, 16 * rng.random((N, 8, 1, V)) ** rng.choice(np.array([2.0, 3.0, 5.0]), (N, 8, 1, 1)))
    price = money(rng, 16 * rng.random((N, 8, 1, P)))
    pool = rng.integers(0, V, (N, 8, 64))
    pop = np.take_along_axis(pool, rng.integers(0, 64, (N, 8, 16 * V)), 2).reshape(N, 8, 16, V)
    kin = np.where(rng.random((N, 8, 16, V)) < 0.15, pop, rng.integers(0, V, (N, 8, 16, V)))
    few = np.take_along_axis(pool, rng.integers(0, 48, (N, 8, P)), 2)
    own = np.where(rng.random((N, 8, P)) < 0.5, few, rng.integers(0, V, (N, 8, P)))
    hold = rng.integers(0, V, (N, 8, P)); wall = rng.integers(0, 2, (N, 8, P)); wt = rng.integers(0, 256, (N, 8, 16))
    return x, kin, own, hold, wall, price, wt
def pack(x, kin, own, hold, wall, price, wt):
    return {"x": np.ascontiguousarray(x.reshape(N, 128, V)).astype(np.float32).astype(BF), "kin": np.ascontiguousarray(kin.reshape(N, 128, V)).astype(np.int32),
            "own": np.stack([gtable(a) for a in own]), "hold": np.stack([gtable(a) for a in hold]), "wall": np.stack([gtable(a) for a in wall]),
            "price": np.ascontiguousarray(price.reshape(N, 128, P)).astype(np.float32).astype(BF), "wt": np.ascontiguousarray(wt.reshape(N, 128, 1)).astype(np.int32)}
def setup_inputs(rng):
    return pack(*parts(rng))
def setup_inputs_alike(rng):
    x, kin, own, hold, wall, price, wt = parts(rng)
    kin[:, 0] = kin[:, 0, :, :1].copy()
    kin[:, 1] = kin[:, 1, :1, :].copy()
    own[:, 2] = own[:, 2, :1].copy()
    kin[:, 3] = rng.integers(0, V, (N, 1, 1))
    own[:, 4] = np.take_along_axis(rng.integers(0, V, (N, 3)), rng.integers(0, 3, (N, P)), 1)
    own[:, 5] = np.argsort(rng.random((N, V)), axis=-1)[:, :P]; price[:, 5] = 15; x[:, 5] = 0; x[:, 5, 3] = rng.integers(0, 2, (N, V))
    own[1::2, 5, P - 1] = own[1::2, 5, 0]; price[1::2, 5, 3, P - 1] = 0
    x[:, 6] = x[:, 6, :, :1].copy(); hold[:, 6] = hold[:, 6, :1].copy()
    kin[:, 7] = rng.choice(np.array([0, 1, V - 2, V - 1]), (N, 16, V)); own[:, 7] = rng.choice(np.array([0, V - 1]), (N, P))
    return pack(x, kin, own, hold, wall, price, wt)
def setup_inputs_corners(rng):
    x, kin, own, hold, wall, price, wt = parts(rng); q = rng.permutation(8); a = np.arange(V)
    for r in range(N):
        g = q[0]; x[r, g] = 0; price[r, g] = 15; kin[r, g] = np.minimum(a + 1, V - 1); own[r, g, ::8] = V - 1; own[r, g, 1::8] = 0; own[r, g, 2::8] = V - 2
        g = q[1]; kin[r, g] = a; own[r, g, :2] = 0; own[r, g, P - 2:] = V - 1
        g = q[2]; price[r, g] = 0; wt[r, g] = 255 * (r % 2)
        g = q[3]; x[r, g] = 15; price[r, g] = 15; wt[r, g] = 255; wall[r, g] = 1; hold[r, g, ::2] = V - 1; hold[r, g, 1::4] = 0
        kin[r, g, 0] = rng.permutation(V); own[r, g] = rng.permutation(V)[:P]
        if r % 2 == 1: own[r, g, P - 1] = own[r, g, 0]; price[r, g, :, P - 1] = 7
        g = q[4 + r % 4]; kin[r, g] = rng.integers(0, 2, (16, V)) * (V - 1); own[r, g] = rng.integers(0, 2, P) * (V - 1)
        g = q[4 + (r + 1) % 4]; wall[r, g] = 0; wt[r, g] = 0
        g = q[4 + (r + 2) % 4]; x[r, g] = 0; x[r, g, :, 0] = 15; price[r, g] = 15; kin[r, g] = np.maximum(a - 1, 0); own[r, g] = rng.integers(0, 2 * T, P)
        g = q[4 + (r + 3) % 4]; wall[r, g] = 1; hold[r, g] = rng.integers(0, 2, P) * (V - 1); kin[r, g, :, V - 1] = 0; kin[r, g, :, 0] = V - 1
    return pack(x, kin, own, hold, wall, price, wt)
def setup_inputs_ends(rng):
    def rec(n):
        k = rng.random((N, 8, 1, n)); el = rng.integers(0, 2, (N, 8, 16, n))
        return 15 * np.where(k < 0.35, 0, np.where(k < 0.7, 1, el))
    x = rec(V); price = rec(P)
    kin = np.where(rng.random((N, 8, 1, V)) < 0.7, rng.integers(0, 2, (N, 8, 16, V)) * (V - 1), rng.integers(0, V, (N, 8, 16, V)))
    own = np.where(rng.random((N, 8, P)) < 0.7, rng.integers(0, 2, (N, 8, P)) * (V - 1), rng.integers(0, V, (N, 8, P)))
    hold = np.where(rng.random((N, 8, P)) < 0.75, rng.integers(0, 2, (N, 8, P)) * (V - 1), rng.integers(0, V, (N, 8, P)))
    wall = rng.integers(0, 2, (N, 8, P)); wt = 255 * rng.integers(0, 2, (N, 8, 16)); wt[N - 1, 7] = 255; wt[N - 1, 0, 0] = 0
    for g in range(8):
        x[:, g, :, 0] = (0, 15, 0, 15)[g % 4]; x[:, g, :, V - 1] = (15, 0, 0, 15)[g % 4]
    x[:, 7, :, 0] = 0; x[:, 7, :, 4] = 0; x[:, 7, :, V - 1] = 15
    kin[:, 7, :, V - 1] = V - 1; kin[:, 7, :, 0] = 0; kin[:, 7, 0::2, 2] = 4; kin[:, 7, 1::2, 2] = 0
    own[:, 7, 0] = V - 1; price[:, 7, :, 0] = 0; wall[:, 7, 0] = 0
    own[:, 7, P - 8:] = V - 1; hold[:, 7, P - 8:] = V - 1; wall[:, 7, P - 8:] = 1
    own[:, 7, P - 16:P - 8] = 0; own[:, 7, P - 24:P - 16] = 2; price[:, 7, :, P - 24:] = 15
    x[:, 5, :, V - 2] = 0; kin[:, 5, :, V - 2] = V - 2; own[:, 5, P - 2:] = V - 2; wall[:, 5, P - 2:] = 0; price[:, 5, :, P - 2:] = 15
    y = 15 >> (T // TL); s = [a for a in range(V, 61201, M) if a % y == 0][0] // y
    for r in range(N):
        wt[r, 5] = rng.permutation(np.array([255] * (s // 255) + [s % 255] + [0] * (15 - s // 255)))
    return pack(x, kin, own, hold, wall, price, wt)
def setup_inputs_spread(rng):
    def skew(top, p, *shape):
        return np.minimum(np.floor(top * rng.random(shape) ** p), top - 1).astype(np.int64)
    x = skew(16, np.exp2(rng.integers(-2, 4, (N, 8, 1, V)) + rng.integers(0, 2, (N, 8, 16, 1))), N, 8, 16, V)
    price = skew(16, np.exp2(rng.integers(-3, 3, (N, 8, 1, P)) + rng.integers(0, 2, (N, 8, 16, 1))), N, 8, 16, P)
    kin = skew(V, np.exp2(rng.integers(-1, 4, (N, 8, 16, 1))), N, 8, 16, V)
    own = skew(V, np.exp2(rng.integers(-2, 4, (N, 8, 1))), N, 8, P); hold = skew(V, np.exp2(rng.integers(-3, 4, (N, 8, 1))), N, 8, P)
    wall = (rng.random((N, 8, P)) < rng.choice(np.array([0.1, 0.5, 0.9]), (N, 8, 1))).astype(np.int64)
    wt = np.minimum(np.floor(np.exp2(8.02 * rng.random((N, 8, 16)))).astype(np.int64) - 1, 255)
    return pack(x, kin, own, hold, wall, price, wt)
def setup_inputs_ties(rng):
    x, kin, own, hold, wall, price, wt = parts(rng)
    n = Q - 2 + rng.integers(0, 2, (N, 8, 1, V)) + (rng.random((N, 8, 1, V)) < 0.03) + (np.arange(8) % 2).reshape(1, 8, 1, 1)
    x = 6 + (np.argsort(rng.random((N, 8, 16, V)), axis=2) < n).astype(np.int64)
    price = np.broadcast_to(rng.choice(np.array([6, 7, 7, 7, 7, 7, 7, 8]), (N, 8, 1, P)), (N, 8, 16, P)).copy()
    i = int(rng.integers(0, 16)); x[:, 6, :, V - 1] = 11; x[:, 6, i, V - 1] = 1
    k6 = kin[:, 6]; k6[k6 == V - 1] = V - 2; kin[:, 6, :, V - 1] = V - 1
    o6 = own[:, 6]; o6[o6 == V - 1] = 0; own[:, 6, P - 2:] = V - 1; wall[:, 6] = 0; price[:, 6, :, P - 2:] = 15
    ya, yz = 15, 15
    for _ in range(T // TL):
        ya, yz = (ya + 11) >> 1, (yz + 1) >> 1
    for r in range(N):
        s = 32768 if r % 2 == 0 else 7 * M
        c = [a for a in range(256) if (s - yz * a) % ya == 0][0]; rest = (s - yz * c) // ya
        wt[r, 6] = np.insert(rng.permutation(np.array([255] * (rest // 255) + [rest % 255] + [0] * (14 - rest // 255))), i, c)
    return pack(x, kin, own, hold, wall, price, wt)
def check_inputs(d):
    bad = []
    for k, hi in (("x", 15), ("kin", V - 1), ("own", V - 1), ("hold", V - 1), ("wall", 1), ("price", 15), ("wt", 255)):
        a = np.asarray(d[k]).astype(np.float64)
        if not (np.min(a) >= 0 and np.max(a) <= hi): bad.append("range of " + k)
        elif np.any(a != np.floor(a)): bad.append("whole numbers in " + k)
    return bad
def reference(x, kin, own, hold, wall, price, wt):
    X = x.astype(np.float32).astype(np.int32).reshape(N, 8, 16, V); K = kin.astype(np.int64).reshape(N, 8, 16, V)
    heir = np.tile(np.arange(V), (N, 8, 1)); lane = np.arange(P)
    e = np.stack([gentries(a) for a in own]).astype(np.int64); h = np.stack([gentries(a) for a in hold]).astype(np.int64); wl = np.stack([gentries(a) for a in wall])
    y = price.astype(np.float32).astype(np.int32).reshape(N, 8, 16, P); w = wt.astype(np.int64).reshape(N, 8, 16, 1)
    for t in range(T):
        for r in range(N):
            s = (r + t) % N; XS, KS, HS, ys, hs, es = X[s], K[s], heir[s], y[r], h[r], e[r].copy()
            c = np.take_along_axis(KS, es[:, None, :], 2)
            d = np.take_along_axis(XS, c.reshape(8, 1, 16 * P), 2).reshape(8, 16, 16, P) - ys[:, :, None, :]
            solvent = np.add.reduce((d >= 0).astype(np.int32), axis=1) >= Q; score = np.add.reduce(np.abs(d), axis=1)
            offers = np.any(solvent, axis=1)
            k = np.where(offers, np.argmax(solvent, axis=1), np.argmin(score, axis=1))
            b = np.take_along_axis(c, k[:, None, :], 1)[:, 0]
            key = np.where(offers, b, V + es)
            first = np.argmax(key[:, :, None] == key[:, None, :], axis=2) == lane
            fg, fp = np.nonzero(first & ~offers); ef, f = es[fg, fp], b[fg, fp]
            KS[fg, 1::2, ef] = KS[fg, 1::2, f]
            HS[fg, ef] = f
            wg, wp = np.nonzero(first & offers); cw = b[wg, wp]
            XS[wg, :, cw] = np.maximum(XS[wg, :, cw] - (ys[wg, :, wp] >> 2), 0)
            ys[wg, :, wp] = np.minimum(ys[wg, :, wp] + 1, 15); hs[wg, wp] = cw
            es = np.take_along_axis(HS, es, 1)
            if t % TL == TL - 1:
                es = np.where(wl[r] == 1, hs, es)
                y[r] = (ys + np.take_along_axis(XS, es[:, None, :], 2)) >> 1
                u = np.add.reduce(w[s] * y[r], axis=1) & (M - 1)
                h[r] = np.where(u >= V, u - V, u)
            e[r] = es
    yk = np.add.reduce(K * np.arange(1, 17).reshape(1, 1, 16, 1), axis=2)
    return {"yx": X.reshape(N, 128, V).astype(np.float32).astype(BF), "yk": yk.astype(np.float32), "yh": heir.astype(np.float32), "yo": e.astype(np.float32), "yt": h.astype(np.float32)}

@@ -1,0 +1,469 @@
+from concourse.mybir import dt, AluOpType, AxisListType, ActivationFunctionType
+
+V, P, NS, FB = 2560, 192, 4, 2752
+W = V + P
+CH = [(0, 7), (7, 14), (14, 16)]
+SG = [(0, 1), (1, 3), (3, 7), (7, 10), (10, 14), (14, 16)]
+BIG, LOW = 2.0 ** 21, 2.0 ** 23
+A = AluOpType
+F = ActivationFunctionType
+
+SCRATCH = {}
+
+
+def _b(name, cols, d, where="sbuf"):
+    SCRATCH[name] = (where, [128] + (cols if isinstance(cols, list) else [cols]), d)
+
+
+for _n, _c in (("Kw", W), ("Hw", W), ("Yw", W), ("ramp", 5312), ("cb", 224), ("tr", 416), ("cTf", 192), ("DM", 192), ("SEG", 192),
+               ("jlrow", 192), ("C3", 192), ("c3t", 192), ("sc3", 192), ("IDF", 128), ("mrow", 128),
+               ("K4", 192), ("K4c", 192), ("keys", 192), ("t1", 192), ("sc", 192), ("bF", 192), ("Fo", 192), ("ce", 192),
+               ("hm", 192), ("DUM", 12), ("DUMF", 12), ("dm0", 12), ("cols", 16), ("eF", 12), ("eB", 12), ("fe", 12),
+               ("dk", 12), ("dkB", 12), ("ek", 12), ("bx", 12), ("oX", 12), ("bk", 12), ("oK", 12), ("wF", 12), ("th", 12), ("hW", 12),
+               ("Aw", 12), ("nw", 12), ("m12", 12), ("eh", 12), ("fin", 24), ("rfin", 24), ("outf", 384), ("WKB", 128),
+               ("yv2", 192), ("yv3", 192), ("gg", 12)):
+    _b(_n, _c, "float32")
+for _n, _c in (("Xw", W), ("d", 3072), ("aa", 3072), ("sg", 3072), ("eq", [12, 192]), ("LA", 2048), ("LB", 2048), ("lv", 2048), ("BO", 128),
+               ("U", 128), ("BW", 128), ("grow", 128), ("irow", 128), ("gt", 128), ("KC", 192), ("zero", 192), ("q", 192), ("ID", 128),
+               ("NID", 128), ("ZB", 96), ("Xb", 192), ("xr", 192), ("pw", 192), ("pj", 192), ("ph", 192)):
+    _b(_n, _c, "bfloat16")
+for _n, _c in (("ki", V), ("own_s", 12), ("hold_s", 12), ("wall_s", 12), ("wt_s", 1), ("ci", 4), ("kI", 12), ("jI", 12),
+               ("KEY", 12), ("bI", 12), ("sI", 12), ("uI", 12)):
+    _b(_n, _c, "int32")
+for _n, _c in (("SELu", 12), ("cTu", 192), ("bU", 12), ("dkU", 12), ("dkf", 192), ("oKu0", 12), ("oKu1", 12), ("oXu", 12), ("wU", 12), ("rU", 24)):
+    _b(_n, _c, "uint16")
+for _t in range(NS):
+    _b("E%d" % _t, 12, "uint16")
+    _b("EO%d" % _t, 12, "uint16")
+    _b("PR%d" % _t, 768, "bfloat16")
+    _b("PO%d" % _t, 192, "bfloat16")
+    _b("HW%d" % _t, 36, "float32")
+for _n, _c in (("Z0", 512), ("Z1", 512), ("Z2", 512), ("CN", 512), ("SS", 512), ("XB", 512), ("Y0", 512), ("Y1", 512)):
+    _b(_n, _c, "float32", "psum")
+
+SEMAPHORES = ["qV", "qS", "qT", "qG", "ls"] + ["dm%d" % i for i in range(24)] + ["r%s%d" % (a, t) for a in "eph" for t in range(1, NS)] + ["rf"]
+
+
+def rank_program(g, core, T, topo):
+    rank = T.rank_of(core)
+    if rank is None:
+        return
+    cores = T.cores
+    n = len(cores)
+    eng = {"V": g.vector, "S": g.scalar, "T": g.tensor, "G": g, "Y": g.sync}
+    cnt = {"V": 0, "S": 0, "T": 0, "G": 0}
+    log = {}
+    known = {q: {} for q in "VSTGY"}
+    clock = {}
+    ndma = [0]
+    psum = ("Z0", "Z1", "Z2", "CN", "SS", "XB", "Y0", "Y1")
+
+    def B(name, lo=0, hi=None, step=1, parts=None):
+        t = T[name]
+        if hi is None:
+            hi = SCRATCH[name][1][1]
+        if parts is None:
+            ap = t[:, lo:hi] if step == 1 else t[:, lo:hi:step]
+        else:
+            ap = t[parts[0]:parts[1]:parts[2], lo:hi]
+        return (ap, [(name, lo, hi)], [])
+
+    def IND(win, off):
+        return (win[0].indirect(off[0]), win[1], off[1])
+
+    def ext(ap):
+        return (ap, [], [])
+
+    def need(q, reads, writes, acc):
+        want = {}
+        for regs, wr in ((reads, False), (writes, True)):
+            for nm, lo, hi in regs:
+                if nm in psum:
+                    lo, hi = 0, 512
+                for e in log.get(nm, []):
+                    if e[0] < hi and lo < e[1] and (wr or e[3]):
+                        if e[4] == q and (not e[3] or acc):
+                            continue
+                        s, v = e[2]
+                        if want.get(s, 0) < v:
+                            want[s] = v
+        for s in sorted(want):
+            v = want[s]
+            if known[q].get(s, 0) >= v:
+                continue
+            eng[q].wait_ge(T.sem[s], v)
+            for k, w in clock.get((s, v), {}).items():
+                if known[q].get(k, 0) < w:
+                    known[q][k] = w
+            known[q][s] = max(known[q].get(s, 0), v)
+
+    def note(q, tok, reads, writes):
+        clock[tok] = dict(known[q])
+        for regs, wr in ((reads, False), (writes, True)):
+            for nm, lo, hi in regs:
+                if nm in psum:
+                    lo, hi = 0, 512
+                lst = log.get(nm, [])
+                if wr:
+                    lst = [e for e in lst if not (lo <= e[0] and e[1] <= hi)]
+                else:
+                    lst = [e for e in lst if not (e[4] == q and not e[3] and lo <= e[0] and e[1] <= hi)]
+                lst.append([lo, hi, tok, wr, q])
+                log[nm] = lst
+
+    def op(q, fn, out, ins, acc=False, done=True):
+        reads = list(out[2])
+        for i in ins:
+            reads += i[1] + i[2]
+        need(q, reads, out[1], acc)
+        inst = fn()
+        s = "q" + q
+        if done:
+            cnt[q] += 1
+            inst.then_inc(T.sem[s], 1)
+            note(q, (s, cnt[q]), reads, out[1])
+        else:
+            note(q, (s, cnt[q] + 1), reads, out[1])
+
+    def dma(q, out, in_):
+        need(q, in_[1], out[1], False)
+        s = "dm%d" % ndma[0]
+        ndma[0] += 1
+        eng[q].dma_start(out[0], in_[0]).then_inc(T.sem[s], 16)
+        known[s] = dict(known[q])
+        note(s, (s, 16), in_[1], out[1])
+
+    sent = [0]
+
+    def send(dst, out, in_, sem, ne):
+        need("G", in_[1], [], False)
+        rid, pid, _ = topo.addr(dst)
+        es = topo.engines(core, dst)[:ne]
+        g.remote_dma(out[0], in_[0], T.sem[sem], T.sem["ls"], pid, rid, sum(1 << e for e in es))
+        sent[0] += len(es)
+
+    def arrive(name, lo, hi, src, sem, ne):
+        v = len(topo.engines(src, core)[:ne])
+        known[sem] = {}
+        note(sem, (sem, v), [], [(name, lo, hi)])
+
+    def val(x):
+        return x[0] if isinstance(x, tuple) else x
+
+    def opnds(*xs):
+        return [x for x in xs if isinstance(x, tuple)]
+
+    def tcopy(out, in_):
+        op("V", lambda: g.vector.tensor_copy(out[0], in_[0]), out, [in_])
+
+    def tt(out, a, b, o):
+        op("V", lambda: g.vector.tensor_tensor(out[0], a[0], b[0], o), out, [a, b])
+
+    def ts(out, a, s1, o1, s2=None, o2=None):
+        if o2 is None:
+            op("V", lambda: g.vector.tensor_scalar(out[0], a[0], val(s1), None, o1), out, [a] + opnds(s1))
+        else:
+            op("V", lambda: g.vector.tensor_scalar(out[0], a[0], val(s1), val(s2), o1, o2), out, [a] + opnds(s1, s2))
+
+    def scan(out, a, b, o1, o2):
+        op("V", lambda: g.vector.tensor_tensor_scan(out[0], a[0], b[0], 0.0, o1, o2), out, [a, b])
+
+    def fill(out, c):
+        op("V", lambda: g.vector.memset(out[0], c), out, [])
+
+    def act(out, in_, f, bias=0.0, scale=1.0):
+        op("S", lambda: g.scalar.activation(out[0], in_[0], f, bias=val(bias), scale=val(scale)), out, [in_] + opnds(bias, scale))
+
+    def mm(out, l, r, st, sp):
+        op("T", lambda: g.tensor.matmul(out[0], l[0], r[0], st, sp), out, [l, r], acc=not st, done=sp)
+
+    def iota(out, pat, base, cm):
+        op("G", lambda: g.iota(out[0], pat, base, cm, allow_small_or_imprecise_dtypes=True), out, [])
+
+    def col(i):
+        return B("cols", i, i + 1)
+
+    H = V // 2
+    dma("Y", B("own_s"), ext(T.own[:]))
+    dma("S", B("ki", H, V), ext(T.kin[:, H:V]))
+    dma("Y", B("ki", 0, H), ext(T.kin[:, 0:H]))
+    dma("S", B("Xw", H, V), ext(T.x[:, H:V]))
+    dma("Y", B("Xw", 0, H), ext(T.x[:, 0:H]))
+    dma("Y", B("PR0", 0, P), ext(T.price[:]))
+    dma("Y", B("hold_s"), ext(T.hold[:]))
+    dma("Y", B("wall_s"), ext(T.wall[:]))
+    dma("Y", B("wt_s"), ext(T.wt[:]))
+
+    iota(B("cols", 9, 10), [[0, 1]], 0, 1)
+    iota(B("dm0"), [[16, 12]], V, 1)
+    iota(B("grow"), [[1, 8], [0, 16]], 0, 0)
+    iota(B("irow"), [[0, 8], [1, 16]], 0, 0)
+    iota(B("K4"), [[4096, 16], [0, 12]], -65536, 0)
+    iota(B("mrow"), [[1, 128]], 0, 0)
+    iota(B("jlrow"), [[0, 12], [1, 16]], 0, 0)
+    iota(B("lv"), [[-16, 16], [1, 8], [16, 16]], 0, 0)
+    RB = 1328
+    iota(B("ramp", 0, RB), [[1, RB]], 0, 0)
+    ci = lambda i: B("ci", i, i + 1)
+    fill(B("cb"), 0.0)
+    fill(B("zero"), 0.0)
+    fill(B("ZB"), -128.0)
+    tcopy(ci(0), col(9))
+    ts(ci(1), ci(0), 4, A.logical_shift_right)
+    ts(ci(2), ci(0), 1, A.bitwise_and)
+    ts(ci(3), ci(0), 4, A.logical_shift_right, 1, A.bitwise_and)
+    ts(ci(0), ci(0), 15, A.bitwise_and)
+    tcopy(B("cols", 0, 3), B("ci", 0, 3))
+    tcopy(col(6), ci(3))
+    ts(col(3), col(2), -1.0, A.mult, 1.0, A.add)
+    ts(col(4), col(1), -16.0, A.mult)
+    ts(col(5), col(0), 1.0, A.add)
+    ts(B("DUM"), B("dm0"), col(4), A.add)
+    ts(B("DUMF"), B("DUM"), float(FB), A.add)
+    ts(B("m12"), B("DUM"), -float(V), A.add)
+    ts(B("kI"), B("m12"), 1.0 / 12.0, A.mult, -11.0 / 24.0, A.add)
+    ts(B("eh"), B("kI"), -12.0, A.mult)
+    tt(B("eh"), B("eh"), B("m12"), A.add)
+    ts(B("jI"), B("eh"), col(6), A.add)
+    ts(B("jI"), B("jI"), 1, A.bitwise_and)
+    ts(B("bx"), B("jI"), 208.0, A.mult)
+    ts(B("bk"), B("eh"), 16.0, A.mult)
+    tt(B("bk"), B("bk"), B("kI"), A.add)
+    tt(B("bk"), B("bk"), B("bx"), A.add)
+    tcopy(B("SELu"), B("bk"))
+    ts(B("BO"), B("grow"), col(1), A.is_equal, 8192.0, A.mult)
+    ts(B("gt"), B("irow"), col(0), A.is_gt)
+    tt(B("U"), B("BO"), B("gt"), A.mult)
+    ts(B("KC"), B("K4"), 1.0 / 131072.0, A.mult)
+    tcopy(B("XB", 192, 384), B("K4"))
+    ts(B("IDF"), B("mrow"), col(9), A.is_equal)
+    ts(B("ID"), B("mrow"), col(9), A.is_equal)
+    ts(B("NID"), B("ID"), -1.0, A.mult)
+    ts(B("DM"), B("jlrow"), col(0), A.is_equal)
+    ts(B("SEG"), B("jlrow"), 0.0, A.is_gt)
+    ts(B("c3t"), B("jlrow"), col(0), A.is_lt, -LOW, A.mult)
+    ts(B("C3"), B("jlrow"), col(0), A.is_equal, BIG, A.mult)
+    tt(B("C3"), B("C3"), B("c3t"), A.add)
+    ts(col(8), col(0), 0.0, A.is_equal, -LOW, A.mult)
+    ts(B("c3t"), B("jlrow"), 15.0, A.is_equal, col(8), A.mult)
+    tt(B("C3"), B("C3"), B("c3t"), A.add)
+    ts(col(11), col(8), -1.0, A.mult, -BIG, A.add)
+    ts(col(10), col(11), float(FB), A.add)
+    ts(B("LA"), B("lv"), col(1), A.is_equal, 65536.0, A.mult)
+    ts(B("LB"), B("LA"), 512.0, A.mult)
+    tcopy(B("E0"), B("own_s"))
+
+    DIAG = (T.eq[:, :, 0:16], [("eq", 0, 192)], [])
+    nxt = cores[(rank + 1) % n]
+    prv = cores[(rank - 1) % n]
+    NE, NP = 16, 16
+    late = []
+
+    def sums(i):
+        y = "Y%d" % (i % 2)
+        mm(B(y, 0, 512), B("WKB"), B("Kw", 512 * i, 512 * i + 512), True, True)
+
+    def sums_out(i):
+        y = "Y%d" % (i % 2)
+        act(B("Yw", 512 * i, 512 * i + 512), B(y, 0, 512), F.Copy)
+
+    for t in range(NS):
+        jub = t % 2 == 1
+        EU, PR, HW, OK = "E%d" % t, "PR%d" % t, "HW%d" % t, "oKu%d" % (t % 2)
+        EO, PO, HN = "EO%d" % t, "PO%d" % t, "HW%d" % (t + 1)
+        if t:
+            arrive(EU, 0, 12, prv, "re%d" % t, NE)
+            arrive(PR, 0, P, prv, "rp%d" % t, NP)
+            arrive(HW, 0, 24 if t == 2 else 36, prv, "rh%d" % t, NE)
+        tcopy(B("cb", 16, 208), IND(B("Kw" if t else "ki", 0, V), B(EU)))
+        op("V", lambda: g.vector.transpose(T.tr[:, 0:192], T.cb[:, 16:208]), B("tr", 0, 192), [B("cb", 16, 208)])
+        op("V", lambda: g.vector.transpose(T.tr[:, 192:416], T.cb[:, 0:224]), B("tr", 192, 416), [B("cb")])
+        tcopy(B("cTu"), IND(B("tr"), B("SELu")))
+        act(B("cTf"), IND(B("tr"), B("SELu")), F.Copy)
+        if t == 0:
+            tcopy(B("Kw", 0, H), B("ki", 0, H))
+        if t == 2:
+            sums(0)
+            sums(1)
+            sums_out(0)
+        act(B(PR, 192, 384), B(PR, 0, 192), F.Copy)
+        act(B(PR, 384, 768), B(PR, 0, 384), F.Copy)
+        tt(B("K4c"), B("XB", 192, 384), B("cTf"), A.add)
+        for a, b in SG:
+            tt(B("d", a * P, b * P), IND(B("Xw", 0, V), B("cTu", 12 * a, 12 * b)), B(PR, 0, (b - a) * P), A.subtract)
+            if a == 1:
+                act(B("aa", 0, 3 * P), B("d", 0, 3 * P), F.Abs)
+                act(B("sg", 0, 3 * P), B("d", 0, 3 * P), F.Sign, bias=-0.5, scale=-1.0)
+            elif a > 1:
+                act(B("aa", a * P, b * P), B("d", a * P, b * P), F.Abs)
+            if a in (3, 10, 14):
+                lo = 7 if a == 10 else a
+                ts(B("sg", lo * P, b * P), B("d", lo * P, b * P), 0.0, A.is_lt, -0.5, A.add)
+        act(B("q"), B(PR, 0, P), F.Identity, bias=129.625, scale=0.25)
+        for c, (a, b) in enumerate(CH):
+            z = "Z%d" % c
+            w = 12 * (b - a)
+            mm(B(z, 0, w), B("BO"), B("KC", 12 * a, 12 * b), True, False)
+            mm(B(z, 0, w), B("IDF"), B("cTf", 12 * a, 12 * b), False, False)
+
+            def rows_a():
+                for j in range(16):
+                    mm(B(z, 0, w), B("LA", 128 * j, 128 * j + 128), B("aa", a * P + j, b * P, 16), False, j == 15)
+
+            def rows_b():
+                mm(B(z, 128, 128 + w), B("BO"), B("ZB", 0, w), True, False)
+                for j in range(16):
+                    mm(B(z, 128, 128 + w), B("LB", 128 * j, 128 * j + 128), B("sg", a * P + j, b * P, 16), False, j == 15)
+            rows_a()
+            rows_b()
+            if c == 0:
+                ts(B("eF"), B(EU), float(FB), A.add)
+                ts(B("eB"), B(EU), col(10), A.add)
+                if t == 0:
+                    tcopy(B("HW0", 0, 12), B("hold_s"))
+                    tcopy(B("HW0", 12, 24), B("wall_s"))
+                    tcopy(B("Kw", H, V), B("ki", H, V))
+                    act(B("ramp", RB, 2 * RB), B("ramp", 0, RB), F.Identity, bias=float(RB))
+                    act(B("ramp", 2 * RB, 4 * RB), B("ramp", 0, 2 * RB), F.Identity, bias=float(2 * RB))
+                if jub:
+                    ts(B("wF"), B(HW, 24, 36), float(V), A.is_lt)
+                    tt(B("th"), B(HW, 24, 36), B(HW, 0, 12), A.subtract)
+                    ts(B("nw"), B(HW, 12, 24), -1.0, A.mult, 1.0, A.add)
+                    tt(B("th"), B("th"), B("wF"), A.mult)
+                    tt(B(HW, 0, 12), B("th"), B(HW, 0, 12), A.add)
+                    tt(B("hW"), B(HW, 0, 12), B(HW, 12, 24), A.mult)
+                for f in late:
+                    f()
+                late = []
+            if c == 2:
+                if t == 2:
+                    sums_out(1)
+                    sums(2)
+                    sums_out(2)
+            tt(B("t1", 12 * a, 12 * b), B(z, 128, 128 + w), B("K4c", 12 * a, 12 * b), A.max)
+            if c == 2:
+                tt(B("t1", 168, 180), B("t1", 168, 180), B("keys", 0, 12), A.min)
+            tt(B("keys", 12 * a, 12 * b), B(z, 0, w), B("t1", 12 * a, 12 * b), A.min)
+            if c == 1:
+                tt(B("keys", 0, 84), B("keys", 0, 84), B("keys", 84, 168), A.min)
+                tt(B("keys", 12, 48), B("keys", 12, 48), B("keys", 48, 84), A.min)
+                tt(B("keys", 0, 24), B("keys", 0, 24), B("keys", 24, 48), A.min)
+                tt(B("keys", 0, 12), B("keys", 0, 12), B("keys", 12, 24), A.min)
+        tt(B("KEY"), B("keys", 168, 180), B("keys", 180, 192), A.min)
+        ts(B("bI"), B("KEY"), 4095, A.bitwise_and)
+        tt(B("fe"), B("KEY"), B("eF"), A.min)
+        tt(B("dk"), B("fe"), B("bI"), A.max)
+        tcopy(B("dkU"), B("dk"))
+        tcopy(B("bU"), B("bI"))
+        tcopy(B("dkf"), IND(B("ramp"), B("dkU")))
+        act(B("bF"), IND(B("ramp", 0, V), B("bU")), F.Copy)
+        act(B("Xb"), IND(B("Xw", 0, V), B("bU")), F.Copy)
+        act(B("Fo"), IND(B("Kw", 0, V), B("bU")), F.Identity, scale=col(2))
+        act(B("ce"), B("cb", 16, 208), F.Identity, scale=col(3))
+        if t == 0:
+            act(B("Hw", 0, V), B("ramp", 0, V), F.Copy)
+        mm(B("CN", 0, P), B("BO"), B("zero"), True, False)
+        for j in range(12):
+            w = P - 16 * j
+            op("V", lambda: g.vector.tensor_scalar(T.eq[:, j, 0:w], T.dkf[:, 16 * j:P], T.dk[:, j:j + 1], None, A.is_equal),
+               (None, [("eq", 16 * j, 16 * j + 16)], []), [B("dkf"), B("dk")])
+            if j < 11:
+                mm(B("CN", 16 * j + 16, P), B("BO"), (T.eq[:, j, 16:w], [("eq", 16 * j, 16 * j + 16)], []), False, False)
+        mm(B("CN", 0, P), B("U"), DIAG, False, True)
+        mm(B("XB", 0, P), B("ID"), B("Xb"), True, False)
+        mm(B("XB", 0, P), B("NID"), B("q"), False, True)
+        if t == 2:
+            sums(3)
+            sums(4)
+            sums_out(3)
+        if t >= 2:
+            yv = "yv%d" % t
+            mm(B("Y1", 0, P), B("WKB"), B("Fo"), True, False)
+            mm(B("Y1", 0, P), B("WKB"), B("ce"), False, True)
+        act(B("xr"), B("XB", 0, P), F.Relu, bias=130.0)
+        if t == 2:
+            sums_out(4)
+        if t >= 2:
+            act(B(yv), B("Y1", 0, P), F.Copy)
+        ts(B("ek"), B("KEY"), 0.0, A.is_lt, 8192.0, A.mult)
+        ts(B("dkB"), B("dk"), col(11), A.add)
+        tt(B("ek"), B("ek"), B("eB"), A.add)
+        if jub:
+            tt(B("th"), B("bI"), B(HW, 0, 12), A.subtract)
+            tt(B("th"), B("th"), B(HW, 12, 24), A.mult)
+        scan(B("sc3"), B("CN", 0, P), B("C3"), A.max, A.add)
+        oX = B("oX") if jub else B(HW, 24, 36)
+        tt(B("bk"), B("sc3", 15, P, 16), B("ek"), A.add)
+        tt(B("bx"), B("sc3", 15, P, 16), B("dkB"), A.add)
+        tt(B("oK"), B("bk"), B("DUMF"), A.min)
+        tt(oX, B("bx"), B("DUM"), A.min)
+        ts(B(OK), B("oK"), float(FB), A.subtract)
+        ts(B("wU"), oX, float(V), A.is_lt)
+        tcopy(IND(B("Hw"), B(OK)), B("bF"))
+        if t == NS - 1:
+            dma("Y", ext(T.yh[:]), B("Hw", 0, V, parts=(0, 128, 16)))
+        if jub:
+            ts(B("wF"), oX, float(V), A.is_lt)
+        tt(B("hm"), IND(B("Hw", 0, V), B(EU)), B("DM"), A.mult)
+        if jub:
+            tt(B("th"), B("th"), B("wF"), A.mult)
+        scan(B("sc"), B("SEG"), B("hm"), A.mult, A.add)
+        el = B("sc", 15, 192, 16)
+        if jub:
+            tt(B("Aw"), B("th"), B("hW"), A.add)
+            tt(B("eh"), el, B("nw"), A.mult)
+            tt(B("fin", 0, 12), B("eh"), B("Aw"), A.add)
+            tcopy(B(EO), B("fin", 0, 12))
+        else:
+            tcopy(B(EO), el)
+        if t < NS - 1:
+            send(nxt, B("E%d" % (t + 1)), B(EO), "re%d" % (t + 1), NE)
+        p2 = "pw" if jub else PO
+        tt(B("pj"), IND(B("ramp", 0, 16), B("wU")), B(PR, 0, P), A.add)
+        tcopy(B("oXu"), oX)
+        ts(B(p2), B("pj"), 15.0, A.min)
+        if not jub:
+            send(nxt, B("PR%d" % (t + 1), 0, P), B(PO), "rp%d" % (t + 1), NP)
+            send(nxt, B(HN), B(HW), "rh%d" % (t + 1), NE)
+            tt(IND(B("Kw"), B(OK)), B("Fo"), B("ce"), A.add)
+        tcopy(IND(B("Xw"), B("oXu")), B("xr"))
+        if t == NS - 1:
+            dma("Y", ext(T.yx[:]), B("Xw", 0, V))
+        if jub:
+            tt(B("pj"), IND(B("Xw", 0, V), B(EO)), B("pw"), A.add)
+            ts(B("ph"), B("pj"), 0.5, A.mult, 129.75, A.add)
+            ts(B(PO), B("ph"), -130.0, A.add)
+            if t < NS - 1:
+                send(nxt, B("PR%d" % (t + 1), 0, P), B(PO), "rp%d" % (t + 1), NP)
+            mm(B("SS", 0, P), B("BW"), B(PO), True, True)
+            if t < NS - 1:
+                tt(IND(B("Kw"), B(OK)), B("Fo"), B("ce"), A.add)
+            scan(B("sc3"), B("SS", 0, P), B("C3"), A.max, A.add)
+            ts(B("sI"), B("sc3", 15, P, 16), col(11), A.add)
+            ts(B("uI"), B("sI"), 4095, A.bitwise_and)
+            ts(B("gg"), B("uI"), float(V), A.is_ge, -float(V), A.mult)
+            if t < NS - 1:
+                tt(B(HW, 0, 12), B("uI"), B("gg"), A.add)
+                send(nxt, B(HN, 0, 24), B(HW, 0, 24), "rh%d" % (t + 1), NE)
+            else:
+                tt(B("fin", 12, 24), B("uI"), B("gg"), A.add)
+                send(cores[(rank - t) % n], B("rfin"), B("fin"), "rf", NE)
+        if t == 0:
+            late = [lambda: tcopy(col(7), B("wt_s")),
+                    lambda: ts(B("WKB"), B("grow"), col(1), A.is_equal, col(5), A.mult),
+                    lambda: ts(B("BW"), B("grow"), col(1), A.is_equal, col(7), A.mult)]
+    tcopy(IND(B("Yw"), B("oKu0")), B("yv2"))
+    tcopy(IND(B("Yw"), B("oKu1")), B("yv3"))
+    dma("Y", ext(T.yk[:]), B("Yw", 0, V, parts=(0, 128, 16)))
+    arrive("rfin", 0, 24, cores[(rank + NS - 1) % n], "rf", NE)
+    tcopy(B("rU"), B("rfin"))
+    tcopy(B("outf", 0, P), IND(B("ramp", 0, V), B("rU", 0, 12)))
+    act(B("outf", P, 2 * P), IND(B("ramp", 0, V), B("rU", 12, 24)), F.Copy)
+    dma("Y", ext(T.yo[:]), B("outf", 0, P, parts=(0, 128, 16)))
+    dma("S", ext(T.yt[:]), B("outf", P, 2 * P, parts=(0, 128, 16)))
+    g.wait_ge(T.sem["ls"], sent[0])
+    for i in range(ndma[0]):
+        g.wait_ge(T.sem["dm%d" % i], 16)
+    for q in "VST":
+        g.wait_ge(T.sem["q" + q], cnt[q])
+    g.wait_ge(T.sem["qG"], cnt["G"])

@@ -2,8 +2,10 @@ from concourse.mybir import dt, AluOpType, AxisListType, ActivationFunctionType
 
 V, P, NS, FB = 2560, 192, 4, 2752
 W = V + P
-CH = [(0, 7), (7, 14), (14, 16)]
-SG = [(0, 1), (1, 3), (3, 7), (7, 10), (10, 14), (14, 16)]
+CH = [(0, 7), (7, 12), (12, 15), (15, 16)]
+C0 = 7
+SG = [(0, 1, None, None, None), (1, 3, 0, 0, None), (3, 7, 3, None, 3), (7, 10, 7, None, None), (10, 12, 10, None, 7),
+      (12, 15, 12, None, 12), (15, 16, 15, None, 15)]
 BIG, LOW = 2.0 ** 21, 2.0 ** 23
 A = AluOpType
 F = ActivationFunctionType
@@ -15,33 +17,33 @@ def _b(name, cols, d, where="sbuf"):
     SCRATCH[name] = (where, [128] + (cols if isinstance(cols, list) else [cols]), d)
 
 
-for _n, _c in (("Kw", W), ("Hw", W), ("Yw", W), ("ramp", 5312), ("cb", 224), ("tr", 416), ("cTf", 192), ("DM", 192), ("SEG", 192),
+for _n, _c in (("Kw", W), ("Hw", W), ("Yw", W), ("ramp", 5312), ("cb", 224), ("tr", 416), ("cTf", 192), ("colj", 16),
                ("jlrow", 192), ("C3", 192), ("c3t", 192), ("sc3", 192), ("IDF", 128), ("mrow", 128),
                ("K4", 192), ("K4c", 192), ("keys", 192), ("t1", 192), ("sc", 192), ("bF", 192), ("Fo", 192), ("ce", 192),
-               ("hm", 192), ("DUM", 12), ("DUMF", 12), ("dm0", 12), ("cols", 16), ("eF", 12), ("eB", 12), ("fe", 12),
+               ("hm", 192), ("DUM", 24), ("bxk", 24), ("dm0", 12), ("cols", 16), ("eF", 12), ("eB", 12), ("fe", 12),
                ("dk", 12), ("dkB", 12), ("ek", 12), ("bx", 12), ("oX", 12), ("bk", 12), ("oK", 12), ("wF", 12), ("th", 12), ("hW", 12),
                ("Aw", 12), ("nw", 12), ("m12", 12), ("eh", 12), ("fin", 24), ("rfin", 24), ("outf", 384), ("WKB", 128),
                ("yv2", 192), ("yv3", 192), ("gg", 12)):
     _b(_n, _c, "float32")
-for _n, _c in (("Xw", W), ("d", 3072), ("aa", 3072), ("sg", 3072), ("eq", [12, 192]), ("LA", 2048), ("LB", 2048), ("lv", 2048), ("BO", 128),
+for _n, _c in (("Xw", W), ("d", 3072), ("aa", 1344), ("sg", 1344), ("as", 3456), ("KZ", 216), ("eq", [12, 192]), ("LA", 2048), ("LB", 2048), ("lv", 128), ("BO", 128),
                ("U", 128), ("BW", 128), ("grow", 128), ("irow", 128), ("gt", 128), ("KC", 192), ("zero", 192), ("q", 192), ("ID", 128),
-               ("NID", 128), ("ZB", 96), ("Xb", 192), ("xr", 192), ("pw", 192), ("pj", 192), ("ph", 192)):
+               ("NID", 128), ("ZB", 96), ("Xb", 192), ("xr", 192), ("pw", 192), ("pj", 192), ("wb", 192), ("ph", 192)):
     _b(_n, _c, "bfloat16")
 for _n, _c in (("ki", V), ("own_s", 12), ("hold_s", 12), ("wall_s", 12), ("wt_s", 1), ("ci", 4), ("kI", 12), ("jI", 12),
                ("KEY", 12), ("bI", 12), ("sI", 12), ("uI", 12)):
     _b(_n, _c, "int32")
-for _n, _c in (("SELu", 12), ("cTu", 192), ("bU", 12), ("dkU", 12), ("dkf", 192), ("oKu0", 12), ("oKu1", 12), ("oXu", 12), ("wU", 12), ("rU", 24)):
+for _n, _c in (("SELu", 12), ("cTu", 192), ("bU", 12), ("dkU", 12), ("dkf", 192), ("of0", 24), ("of1", 24), ("wU", 12), ("rU", 24)):
     _b(_n, _c, "uint16")
 for _t in range(NS):
     _b("E%d" % _t, 12, "uint16")
     _b("EO%d" % _t, 12, "uint16")
     _b("PR%d" % _t, 768, "bfloat16")
     _b("PO%d" % _t, 192, "bfloat16")
-    _b("HW%d" % _t, 36, "float32")
+    _b("HW%d" % _t, 48, "float32")
 for _n, _c in (("Z0", 512), ("Z1", 512), ("Z2", 512), ("CN", 512), ("SS", 512), ("XB", 512), ("Y0", 512), ("Y1", 512)):
     _b(_n, _c, "float32", "psum")
 
-SEMAPHORES = ["qV", "qS", "qT", "qG", "ls"] + ["dm%d" % i for i in range(24)] + ["r%s%d" % (a, t) for a in "eph" for t in range(1, NS)] + ["rf"]
+SEMAPHORES = ["qV", "qS", "qT", "qG", "ls"] + ["dm%d" % i for i in range(24)] + ["r%s%d" % (a, t) for a in "eph" for t in range(1, NS)] + ["rf", "ro1"]
 
 
 def rank_program(g, core, T, topo):
@@ -185,11 +187,9 @@ def rank_program(g, core, T, topo):
 
     H = V // 2
     dma("Y", B("own_s"), ext(T.own[:]))
-    dma("S", B("ki", H, V), ext(T.kin[:, H:V]))
-    dma("Y", B("ki", 0, H), ext(T.kin[:, 0:H]))
-    dma("S", B("Xw", H, V), ext(T.x[:, H:V]))
-    dma("Y", B("Xw", 0, H), ext(T.x[:, 0:H]))
+    dma("Y", B("ki"), ext(T.kin[:]))
     dma("Y", B("PR0", 0, P), ext(T.price[:]))
+    dma("Y", B("Xw", 0, V), ext(T.x[:]))
     dma("Y", B("hold_s"), ext(T.hold[:]))
     dma("Y", B("wall_s"), ext(T.wall[:]))
     dma("Y", B("wt_s"), ext(T.wt[:]))
@@ -201,9 +201,12 @@ def rank_program(g, core, T, topo):
     iota(B("K4"), [[4096, 16], [0, 12]], -65536, 0)
     iota(B("mrow"), [[1, 128]], 0, 0)
     iota(B("jlrow"), [[0, 12], [1, 16]], 0, 0)
-    iota(B("lv"), [[-16, 16], [1, 8], [16, 16]], 0, 0)
+    iota(B("lv"), [[1, 8], [16, 16]], 0, 0)
+    iota(B("colj"), [[16, 16]], 0, 0)
     RB = 1328
     iota(B("ramp", 0, RB), [[1, RB]], 0, 0)
+    act(B("ramp", RB, 2 * RB), B("ramp", 0, RB), F.Identity, bias=float(RB))
+    act(B("ramp", 2 * RB, 4 * RB), B("ramp", 0, 2 * RB), F.Identity, bias=float(2 * RB))
     ci = lambda i: B("ci", i, i + 1)
     fill(B("cb"), 0.0)
     fill(B("zero"), 0.0)
@@ -218,9 +221,9 @@ def rank_program(g, core, T, topo):
     ts(col(3), col(2), -1.0, A.mult, 1.0, A.add)
     ts(col(4), col(1), -16.0, A.mult)
     ts(col(5), col(0), 1.0, A.add)
-    ts(B("DUM"), B("dm0"), col(4), A.add)
-    ts(B("DUMF"), B("DUM"), float(FB), A.add)
-    ts(B("m12"), B("DUM"), -float(V), A.add)
+    ts(B("DUM", 0, 12), B("dm0"), col(4), A.add)
+    ts(B("DUM", 12, 24), B("dm0"), col(4), A.add)
+    ts(B("m12"), B("DUM", 0, 12), -float(V), A.add)
     ts(B("kI"), B("m12"), 1.0 / 12.0, A.mult, -11.0 / 24.0, A.add)
     ts(B("eh"), B("kI"), -12.0, A.mult)
     tt(B("eh"), B("eh"), B("m12"), A.add)
@@ -235,12 +238,14 @@ def rank_program(g, core, T, topo):
     ts(B("gt"), B("irow"), col(0), A.is_gt)
     tt(B("U"), B("BO"), B("gt"), A.mult)
     ts(B("KC"), B("K4"), 1.0 / 131072.0, A.mult)
+    fill(B("KZ"), -2176.0)
+    for a, b in CH[1:]:
+        o = 24 * (a - C0)
+        tcopy(B("KZ", o, o + 12 * (b - a)), B("KC", 12 * a, 12 * b))
     tcopy(B("XB", 192, 384), B("K4"))
     ts(B("IDF"), B("mrow"), col(9), A.is_equal)
     ts(B("ID"), B("mrow"), col(9), A.is_equal)
     ts(B("NID"), B("ID"), -1.0, A.mult)
-    ts(B("DM"), B("jlrow"), col(0), A.is_equal)
-    ts(B("SEG"), B("jlrow"), 0.0, A.is_gt)
     ts(B("c3t"), B("jlrow"), col(0), A.is_lt, -LOW, A.mult)
     ts(B("C3"), B("jlrow"), col(0), A.is_equal, BIG, A.mult)
     tt(B("C3"), B("C3"), B("c3t"), A.add)
@@ -248,9 +253,11 @@ def rank_program(g, core, T, topo):
     ts(B("c3t"), B("jlrow"), 15.0, A.is_equal, col(8), A.mult)
     tt(B("C3"), B("C3"), B("c3t"), A.add)
     ts(col(11), col(8), -1.0, A.mult, -BIG, A.add)
-    ts(col(10), col(11), float(FB), A.add)
-    ts(B("LA"), B("lv"), col(1), A.is_equal, 65536.0, A.mult)
+    ts(B("colj"), B("colj"), col(1), A.add)
+    for j in range(16):
+        ts(B("LA", 128 * j, 128 * j + 128), B("lv"), B("colj", j, j + 1), A.is_equal, 65536.0, A.mult)
     ts(B("LB"), B("LA"), 512.0, A.mult)
+    ts(B("WKB"), B("grow"), col(1), A.is_equal, col(5), A.mult)
     tcopy(B("E0"), B("own_s"))
 
     DIAG = (T.eq[:, :, 0:16], [("eq", 0, 192)], [])
@@ -258,6 +265,13 @@ def rank_program(g, core, T, topo):
     prv = cores[(rank - 1) % n]
     NE, NP = 16, 16
     late = []
+
+    def absd(a, b, sign=False):
+        if a < C0:
+            return B("aa", a * P, b * P)
+        ca, cb = [c for c in CH if c[0] <= a < c[1]][0]
+        o = 2 * (ca - C0) + (a - ca) + (cb - ca if sign else 0)
+        return B("as", o * P, (o + b - a) * P)
 
     def sums(i):
         y = "Y%d" % (i % 2)
@@ -269,12 +283,15 @@ def rank_program(g, core, T, topo):
 
     for t in range(NS):
         jub = t % 2 == 1
-        EU, PR, HW, OK = "E%d" % t, "PR%d" % t, "HW%d" % t, "oKu%d" % (t % 2)
+        EU, PR, HW, OF = "E%d" % t, "PR%d" % t, "HW%d" % t, "of%d" % (t % 2)
+        OX, OK = B(OF, 0, 12), B(OF, 12, 24)
         EO, PO, HN = "EO%d" % t, "PO%d" % t, "HW%d" % (t + 1)
         if t:
             arrive(EU, 0, 12, prv, "re%d" % t, NE)
             arrive(PR, 0, P, prv, "rp%d" % t, NP)
-            arrive(HW, 0, 24 if t == 2 else 36, prv, "rh%d" % t, NE)
+            arrive(HW, 0, 36 if t == 3 else 24, prv, "rh%d" % t, NE)
+            if t == 1:
+                arrive(HW, 24, 36, prv, "ro1", NE)
         tcopy(B("cb", 16, 208), IND(B("Kw" if t else "ki", 0, V), B(EU)))
         op("V", lambda: g.vector.transpose(T.tr[:, 0:192], T.cb[:, 16:208]), B("tr", 0, 192), [B("cb", 16, 208)])
         op("V", lambda: g.vector.transpose(T.tr[:, 192:416], T.cb[:, 0:224]), B("tr", 192, 416), [B("cb")])
@@ -282,86 +299,113 @@ def rank_program(g, core, T, topo):
         act(B("cTf"), IND(B("tr"), B("SELu")), F.Copy)
         if t == 0:
             tcopy(B("Kw", 0, H), B("ki", 0, H))
+            late = [lambda: tcopy(B("HW0", 0, 12), B("hold_s")),
+                    lambda: tcopy(B("HW0", 12, 24), B("wall_s")),
+                    lambda: send(nxt, B("HW1", 0, 24), B("HW0", 0, 24), "rh1", NE),
+                    lambda: tcopy(col(7), B("wt_s")),
+                    lambda: ts(B("BW"), B("grow"), col(1), A.is_equal, col(7), A.mult)]
         if t == 2:
+            late.pop(0)()
             sums(0)
             sums(1)
-            sums_out(0)
+        if t == 1:
+            mm(B("SS", 0, 16), B("BW"), B("ZB", 0, 16), True, True)
+            late = [lambda: ts(col(12), B("SS", 0, 1), 130.0 / 128.0, A.mult, col(11), A.add)]
         act(B(PR, 192, 384), B(PR, 0, 192), F.Copy)
         act(B(PR, 384, 768), B(PR, 0, 384), F.Copy)
-        tt(B("K4c"), B("XB", 192, 384), B("cTf"), A.add)
-        for a, b in SG:
+        side = []
+
+        def fillers():
+            if side:
+                side.pop(0)()
+        for a, b, ab, sn, iv in SG:
             tt(B("d", a * P, b * P), IND(B("Xw", 0, V), B("cTu", 12 * a, 12 * b)), B(PR, 0, (b - a) * P), A.subtract)
-            if a == 1:
-                act(B("aa", 0, 3 * P), B("d", 0, 3 * P), F.Abs)
-                act(B("sg", 0, 3 * P), B("d", 0, 3 * P), F.Sign, bias=-0.5, scale=-1.0)
-            elif a > 1:
-                act(B("aa", a * P, b * P), B("d", a * P, b * P), F.Abs)
-            if a in (3, 10, 14):
-                lo = 7 if a == 10 else a
-                ts(B("sg", lo * P, b * P), B("d", lo * P, b * P), 0.0, A.is_lt, -0.5, A.add)
+            if a == 0:
+                tt(B("K4c"), B("XB", 192, 384), B("cTf"), A.add)
+            if ab is not None:
+                act(absd(ab, b), B("d", ab * P, b * P), F.Abs)
+            if sn is not None:
+                act(B("sg", sn * P, b * P), B("d", sn * P, b * P), F.Sign, bias=-0.5, scale=-1.0)
+            if iv is not None and iv < C0:
+                ts(B("sg", iv * P, b * P), B("d", iv * P, b * P), 0.0, A.is_lt, -0.5, A.add)
+            elif iv is not None:
+                ts(absd(iv, b, True), B("d", iv * P, b * P), 0.0, A.is_lt, 512.0, A.mult)
         act(B("q"), B(PR, 0, P), F.Identity, bias=129.625, scale=0.25)
+        if t == 0:
+            act(B("Hw", 0, V), B("ramp", 0, V), F.Copy)
         for c, (a, b) in enumerate(CH):
-            z = "Z%d" % c
+            z = ("Z0", "Z1", "Z2", "CN")[c]
             w = 12 * (b - a)
-            mm(B(z, 0, w), B("BO"), B("KC", 12 * a, 12 * b), True, False)
-            mm(B(z, 0, w), B("IDF"), B("cTf", 12 * a, 12 * b), False, False)
-
-            def rows_a():
+            zb = w if c else 128
+            if c == 0:
+                mm(B(z, 0, w), B("BO"), B("KC", 0, w), True, False)
+                mm(B(z, 0, w), B("IDF"), B("cTf", 0, w), False, False)
                 for j in range(16):
-                    mm(B(z, 0, w), B("LA", 128 * j, 128 * j + 128), B("aa", a * P + j, b * P, 16), False, j == 15)
-
-            def rows_b():
+                    mm(B(z, 0, w), B("LA", 128 * j, 128 * j + 128), B("aa", j, b * P, 16), False, j == 15)
                 mm(B(z, 128, 128 + w), B("BO"), B("ZB", 0, w), True, False)
                 for j in range(16):
-                    mm(B(z, 128, 128 + w), B("LB", 128 * j, 128 * j + 128), B("sg", a * P + j, b * P, 16), False, j == 15)
-            rows_a()
-            rows_b()
+                    mm(B(z, 128, 128 + w), B("LB", 128 * j, 128 * j + 128), B("sg", j, b * P, 16), False, j == 15)
+            else:
+                lo, hi = 2 * (a - C0), 2 * (b - C0)
+                mm(B(z, 0, 2 * w), B("BO"), B("KZ", 12 * lo, 12 * hi), True, False)
+                mm(B(z, 0, w), B("IDF"), B("cTf", 12 * a, 12 * b), False, False)
+                for j in range(16):
+                    mm(B(z, 0, 2 * w), B("LA", 128 * j, 128 * j + 128), B("as", lo * P + j, hi * P, 16), False, j == 15)
             if c == 0:
-                ts(B("eF"), B(EU), float(FB), A.add)
-                ts(B("eB"), B(EU), col(10), A.add)
+                side = [lambda: ts(B("eF"), B(EU), float(FB), A.add),
+                        lambda: ts(B("eB"), B(EU), col(11), A.add)]
                 if t == 0:
-                    tcopy(B("HW0", 0, 12), B("hold_s"))
-                    tcopy(B("HW0", 12, 24), B("wall_s"))
-                    tcopy(B("Kw", H, V), B("ki", H, V))
-                    act(B("ramp", RB, 2 * RB), B("ramp", 0, RB), F.Identity, bias=float(RB))
-                    act(B("ramp", 2 * RB, 4 * RB), B("ramp", 0, 2 * RB), F.Identity, bias=float(2 * RB))
+                    side = [lambda: tcopy(B("Kw", H, V), B("ki", H, V))] + side
                 if jub:
-                    ts(B("wF"), B(HW, 24, 36), float(V), A.is_lt)
-                    tt(B("th"), B(HW, 24, 36), B(HW, 0, 12), A.subtract)
-                    ts(B("nw"), B(HW, 12, 24), -1.0, A.mult, 1.0, A.add)
-                    tt(B("th"), B("th"), B("wF"), A.mult)
-                    tt(B(HW, 0, 12), B("th"), B(HW, 0, 12), A.add)
-                    tt(B("hW"), B(HW, 0, 12), B(HW, 12, 24), A.mult)
-                for f in late:
-                    f()
+                    side += [lambda: ts(B("wF"), B(HW, 24, 36), float(V), A.is_lt),
+                             lambda: tt(B("th"), B(HW, 24, 36), B(HW, 0, 12), A.subtract),
+                             lambda: ts(B("nw"), B(HW, 12, 24), -1.0, A.mult, 1.0, A.add),
+                             lambda: tt(B("th"), B("th"), B("wF"), A.mult),
+                             lambda: ts(B("Aw"), B("nw"), col(11), A.mult),
+                             lambda: tt(B(HW, 0, 12), B("th"), B(HW, 0, 12), A.add),
+                             lambda: tt(B("hW"), B(HW, 0, 12), B(HW, 12, 24), A.mult),
+                             lambda: tt(B("hW"), B("hW"), B("Aw"), A.add)]
+                side += late
                 late = []
-            if c == 2:
+            if c == 3:
+                while side:
+                    fillers()
                 if t == 2:
+                    sums_out(0)
                     sums_out(1)
                     sums(2)
-                    sums_out(2)
-            tt(B("t1", 12 * a, 12 * b), B(z, 128, 128 + w), B("K4c", 12 * a, 12 * b), A.max)
+            tt(B("t1", 12 * a, 12 * b), B(z, zb, zb + w), B("K4c", 12 * a, 12 * b), A.max)
+            if c == 3:
+                tt(B("t1", 180, 192), B("t1", 180, 192), B("keys", 168, 180), A.min)
+                tt(B("KEY"), B(z, 0, w), B("t1", 180, 192), A.min)
+                break
+            fillers()
             if c == 2:
-                tt(B("t1", 168, 180), B("t1", 168, 180), B("keys", 0, 12), A.min)
+                tt(B("t1", 144, 180), B("t1", 144, 180), B("keys", 0, 36), A.min)
+                fillers()
             tt(B("keys", 12 * a, 12 * b), B(z, 0, w), B("t1", 12 * a, 12 * b), A.min)
+            fillers()
             if c == 1:
-                tt(B("keys", 0, 84), B("keys", 0, 84), B("keys", 84, 168), A.min)
-                tt(B("keys", 12, 48), B("keys", 12, 48), B("keys", 48, 84), A.min)
-                tt(B("keys", 0, 24), B("keys", 0, 24), B("keys", 24, 48), A.min)
-                tt(B("keys", 0, 12), B("keys", 0, 12), B("keys", 12, 24), A.min)
-        tt(B("KEY"), B("keys", 168, 180), B("keys", 180, 192), A.min)
+                tt(B("keys", 0, 72), B("keys", 0, 72), B("keys", 72, 144), A.min)
+                fillers()
+                tt(B("keys", 0, 36), B("keys", 0, 36), B("keys", 36, 72), A.min)
+                fillers()
+            if c == 2:
+                tt(B("keys", 144, 156), B("keys", 144, 156), B("keys", 156, 168), A.min)
+                fillers()
+                tt(B("keys", 168, 180), B("keys", 144, 156), B("keys", 168, 180), A.min)
         ts(B("bI"), B("KEY"), 4095, A.bitwise_and)
         tt(B("fe"), B("KEY"), B("eF"), A.min)
-        tt(B("dk"), B("fe"), B("bI"), A.max)
-        tcopy(B("dkU"), B("dk"))
         tcopy(B("bU"), B("bI"))
+        tt(B("dk"), B("fe"), B("bI"), A.max)
+        ts(B("ek"), B("KEY"), 0.0, A.is_lt, 8192.0, A.mult)
+        tcopy(B("dkU"), B("dk"))
+        ts(B("dkB"), B("dk"), col(11), A.add)
         tcopy(B("dkf"), IND(B("ramp"), B("dkU")))
         act(B("bF"), IND(B("ramp", 0, V), B("bU")), F.Copy)
         act(B("Xb"), IND(B("Xw", 0, V), B("bU")), F.Copy)
         act(B("Fo"), IND(B("Kw", 0, V), B("bU")), F.Identity, scale=col(2))
         act(B("ce"), B("cb", 16, 208), F.Identity, scale=col(3))
-        if t == 0:
-            act(B("Hw", 0, V), B("ramp", 0, V), F.Copy)
         mm(B("CN", 0, P), B("BO"), B("zero"), True, False)
         for j in range(12):
             w = P - 16 * j
@@ -373,87 +417,97 @@ def rank_program(g, core, T, topo):
         mm(B("XB", 0, P), B("ID"), B("Xb"), True, False)
         mm(B("XB", 0, P), B("NID"), B("q"), False, True)
         if t == 2:
+            sums_out(2)
             sums(3)
             sums(4)
+        act(B("xr"), B("XB", 0, P), F.Relu, bias=130.0)
+        tt(B("ek"), B("ek"), B("eB"), A.add)
+        if jub:
+            tt(B("th"), B("bI"), B(HW, 0, 12), A.subtract)
+        scan(B("sc3"), B("CN", 0, P), B("C3"), A.max, A.add)
+        oX = B(HW, 24, 36)
+        tt(B("bxk", 12, 24), B("sc3", 15, P, 16), B("ek"), A.add)
+        tt(B("bxk", 0, 12), B("sc3", 15, P, 16), B("dkB"), A.add)
+        if jub:
+            tt(B("th"), B("th"), B(HW, 12, 24), A.mult)
+        tt(B(HW, 24, 48), B("bxk"), B("DUM"), A.min)
+        tcopy(B(OF), B(HW, 24, 48))
+        ts(B("wU"), oX, float(V), A.is_lt)
+        tcopy(IND(B("Hw"), OK), B("bF"))
+        act(B("hm"), IND(B("Hw", 0, V), B(EU)), F.Copy)
+        if t == NS - 1:
+            dma("Y", ext(T.yh[:]), B("Hw", 0, V, parts=(0, 128, 16)))
+        if t == 2:
             sums_out(3)
+            sums_out(4)
+        if t == NS - 1:
+            tcopy(IND(B("Xw"), OX), B("xr"))
+            dma("Y", ext(T.yx[:]), B("Xw", 0, V))
+        if jub:
+            act(B("wb"), IND(B("ramp", 0, 16), B("wU")), F.Copy)
+            mm(B("Z2", 0, P), B("ID"), B("wb"), True, False)
+            mm(B("Z2", 0, P), B("ID"), B(PR, 0, P), False, True)
+            act(B("pj"), B("Z2", 0, P), F.Relu, bias=15.0, scale=-1.0)
+            act(B("pw"), B("pj"), F.Identity, bias=15.0, scale=-1.0)
+            ts(B("wF"), oX, float(V), A.is_lt)
+            tt(B("th"), B("th"), B("wF"), A.mult)
+            tt(B("Aw"), B("th"), B("hW"), A.add)
+        else:
+            tt(B("pj"), IND(B("ramp", 0, 16), B("wU")), B(PR, 0, P), A.add)
         if t >= 2:
             yv = "yv%d" % t
             mm(B("Y1", 0, P), B("WKB"), B("Fo"), True, False)
             mm(B("Y1", 0, P), B("WKB"), B("ce"), False, True)
-        act(B("xr"), B("XB", 0, P), F.Relu, bias=130.0)
-        if t == 2:
-            sums_out(4)
-        if t >= 2:
             act(B(yv), B("Y1", 0, P), F.Copy)
-        ts(B("ek"), B("KEY"), 0.0, A.is_lt, 8192.0, A.mult)
-        ts(B("dkB"), B("dk"), col(11), A.add)
-        tt(B("ek"), B("ek"), B("eB"), A.add)
-        if jub:
-            tt(B("th"), B("bI"), B(HW, 0, 12), A.subtract)
-            tt(B("th"), B("th"), B(HW, 12, 24), A.mult)
-        scan(B("sc3"), B("CN", 0, P), B("C3"), A.max, A.add)
-        oX = B("oX") if jub else B(HW, 24, 36)
-        tt(B("bk"), B("sc3", 15, P, 16), B("ek"), A.add)
-        tt(B("bx"), B("sc3", 15, P, 16), B("dkB"), A.add)
-        tt(B("oK"), B("bk"), B("DUMF"), A.min)
-        tt(oX, B("bx"), B("DUM"), A.min)
-        ts(B(OK), B("oK"), float(FB), A.subtract)
-        ts(B("wU"), oX, float(V), A.is_lt)
-        tcopy(IND(B("Hw"), B(OK)), B("bF"))
-        if t == NS - 1:
-            dma("Y", ext(T.yh[:]), B("Hw", 0, V, parts=(0, 128, 16)))
-        if jub:
-            ts(B("wF"), oX, float(V), A.is_lt)
-        tt(B("hm"), IND(B("Hw", 0, V), B(EU)), B("DM"), A.mult)
-        if jub:
-            tt(B("th"), B("th"), B("wF"), A.mult)
-        scan(B("sc"), B("SEG"), B("hm"), A.mult, A.add)
+        scan(B("sc"), B("hm"), B("C3"), A.max, A.add)
         el = B("sc", 15, 192, 16)
         if jub:
-            tt(B("Aw"), B("th"), B("hW"), A.add)
             tt(B("eh"), el, B("nw"), A.mult)
             tt(B("fin", 0, 12), B("eh"), B("Aw"), A.add)
             tcopy(B(EO), B("fin", 0, 12))
         else:
-            tcopy(B(EO), el)
+            ts(B(EO), el, col(11), A.add)
         if t < NS - 1:
             send(nxt, B("E%d" % (t + 1)), B(EO), "re%d" % (t + 1), NE)
-        p2 = "pw" if jub else PO
-        tt(B("pj"), IND(B("ramp", 0, 16), B("wU")), B(PR, 0, P), A.add)
-        tcopy(B("oXu"), oX)
-        ts(B(p2), B("pj"), 15.0, A.min)
         if not jub:
+            ts(B(PO), B("pj"), 15.0, A.min)
             send(nxt, B("PR%d" % (t + 1), 0, P), B(PO), "rp%d" % (t + 1), NP)
-            send(nxt, B(HN), B(HW), "rh%d" % (t + 1), NE)
-            tt(IND(B("Kw"), B(OK)), B("Fo"), B("ce"), A.add)
-        tcopy(IND(B("Xw"), B("oXu")), B("xr"))
-        if t == NS - 1:
-            dma("Y", ext(T.yx[:]), B("Xw", 0, V))
+            if t == 0:
+                send(nxt, B(HN, 24, 36), B(HW, 24, 36), "ro1", NE)
+            else:
+                send(nxt, B(HN, 0, 36), B(HW, 0, 36), "rh%d" % (t + 1), NE)
+            tt(IND(B("Kw"), OK), B("Fo"), B("ce"), A.add)
+        if t < NS - 1:
+            tcopy(IND(B("Xw"), OX), B("xr"))
         if jub:
             tt(B("pj"), IND(B("Xw", 0, V), B(EO)), B("pw"), A.add)
             ts(B("ph"), B("pj"), 0.5, A.mult, 129.75, A.add)
-            ts(B(PO), B("ph"), -130.0, A.add)
+            mm(B("SS", 0, P), B("BW"), B("ph"), True, True)
             if t < NS - 1:
+                ts(B(PO), B("ph"), -130.0, A.add)
                 send(nxt, B("PR%d" % (t + 1), 0, P), B(PO), "rp%d" % (t + 1), NP)
-            mm(B("SS", 0, P), B("BW"), B(PO), True, True)
-            if t < NS - 1:
-                tt(IND(B("Kw"), B(OK)), B("Fo"), B("ce"), A.add)
-            scan(B("sc3"), B("SS", 0, P), B("C3"), A.max, A.add)
-            ts(B("sI"), B("sc3", 15, P, 16), col(11), A.add)
-            ts(B("uI"), B("sI"), 4095, A.bitwise_and)
-            ts(B("gg"), B("uI"), float(V), A.is_ge, -float(V), A.mult)
-            if t < NS - 1:
-                tt(B(HW, 0, 12), B("uI"), B("gg"), A.add)
-                send(nxt, B(HN, 0, 24), B(HW, 0, 24), "rh%d" % (t + 1), NE)
+                tt(IND(B("Kw"), OK), B("Fo"), B("ce"), A.add)
+
+            def holders(t=t, HW=HW, HN=HN):
+                def home():
+                    if t < NS - 1:
+                        tt(B(HW, 0, 12), B("uI"), B("gg"), A.add)
+                        send(nxt, B(HN, 0, 24), B(HW, 0, 24), "rh%d" % (t + 1), NE)
+                    else:
+                        tt(B("fin", 12, 24), B("uI"), B("gg"), A.add)
+                        send(cores[(rank - t) % n], B("rfin"), B("fin"), "rf", NE)
+                return [lambda: scan(B("sc3"), B("SS", 0, P), B("C3"), A.max, A.add),
+                        lambda: ts(B("sI"), B("sc3", 15, P, 16), col(12), A.add),
+                        lambda: ts(B("uI"), B("sI"), 4095, A.bitwise_and),
+                        lambda: ts(B("gg"), B("uI"), float(V), A.is_ge, -float(V), A.mult),
+                        home]
+            if t == NS - 1:
+                for f in holders():
+                    f()
             else:
-                tt(B("fin", 12, 24), B("uI"), B("gg"), A.add)
-                send(cores[(rank - t) % n], B("rfin"), B("fin"), "rf", NE)
-        if t == 0:
-            late = [lambda: tcopy(col(7), B("wt_s")),
-                    lambda: ts(B("WKB"), B("grow"), col(1), A.is_equal, col(5), A.mult),
-                    lambda: ts(B("BW"), B("grow"), col(1), A.is_equal, col(7), A.mult)]
-    tcopy(IND(B("Yw"), B("oKu0")), B("yv2"))
-    tcopy(IND(B("Yw"), B("oKu1")), B("yv3"))
+                late = holders()
+    tcopy(IND(B("Yw"), B("of0", 12, 24)), B("yv2"))
+    tcopy(IND(B("Yw"), B("of1", 12, 24)), B("yv3"))
     dma("Y", ext(T.yk[:]), B("Yw", 0, V, parts=(0, 128, 16)))
     arrive("rfin", 0, 24, cores[(rank + NS - 1) % n], "rf", NE)
     tcopy(B("rU"), B("rfin"))

from concourse.mybir import dt, AluOpType, AxisListType, ActivationFunctionType

V, P, NS, FB = 2560, 192, 4, 2752
W = V + P
CH = [(0, 7), (7, 12), (12, 15), (15, 16)]
C0 = 7
SG = [(0, 1, None, None, None), (1, 3, 0, 0, None), (3, 7, 3, None, 3), (7, 10, 7, None, None), (10, 12, 10, None, 7),
      (12, 15, 12, None, 12), (15, 16, 15, None, 15)]
BIG, LOW = 2.0 ** 21, 2.0 ** 23
A = AluOpType
F = ActivationFunctionType

SCRATCH = {}


def _b(name, cols, d, where="sbuf"):
    SCRATCH[name] = (where, [128] + (cols if isinstance(cols, list) else [cols]), d)


for _n, _c in (("Kw", W), ("Hw", W), ("Yw", W), ("ramp", 5312), ("cb", 224), ("tr", 416), ("cTf", 192), ("colj", 16),
               ("jlrow", 192), ("C3", 192), ("c3t", 192), ("sc3", 192), ("IDF", 128), ("mrow", 128),
               ("K4", 192), ("K4c", 192), ("keys", 192), ("t1", 192), ("sc", 192), ("bF", 192), ("Fo", 192), ("ce", 192),
               ("hm", 192), ("DUM", 24), ("bxk", 24), ("dm0", 12), ("cols", 16), ("eF", 12), ("eB", 12), ("fe", 12),
               ("dk", 12), ("dkB", 12), ("ek", 12), ("bx", 12), ("oX", 12), ("bk", 12), ("oK", 12), ("wF", 12), ("th", 12), ("hW", 12),
               ("Aw", 12), ("nw", 12), ("m12", 12), ("eh", 12), ("fin", 24), ("rfin", 24), ("outf", 384), ("WKB", 128),
               ("yv2", 192), ("yv3", 192), ("gg", 12)):
    _b(_n, _c, "float32")
for _n, _c in (("Xw", W), ("d", 3072), ("aa", 1344), ("sg", 1344), ("as", 3456), ("KZ", 216), ("eq", [12, 192]), ("LA", 2048), ("LB", 2048), ("lv", 128), ("BO", 128),
               ("U", 128), ("BW", 128), ("grow", 128), ("irow", 128), ("gt", 128), ("KC", 192), ("zero", 192), ("q", 192), ("ID", 128),
               ("NID", 128), ("ZB", 96), ("Xb", 192), ("xr", 192), ("pw", 192), ("pj", 192), ("wb", 192), ("ph", 192)):
    _b(_n, _c, "bfloat16")
for _n, _c in (("ki", V), ("own_s", 12), ("hold_s", 12), ("wall_s", 12), ("wt_s", 1), ("ci", 4), ("kI", 12), ("jI", 12),
               ("KEY", 12), ("bI", 12), ("sI", 12), ("uI", 12)):
    _b(_n, _c, "int32")
for _n, _c in (("SELu", 12), ("cTu", 192), ("bU", 12), ("dkU", 12), ("dkf", 192), ("of0", 24), ("of1", 24), ("wU", 12), ("rU", 24)):
    _b(_n, _c, "uint16")
for _t in range(NS):
    _b("E%d" % _t, 12, "uint16")
    _b("EO%d" % _t, 12, "uint16")
    _b("PR%d" % _t, 768, "bfloat16")
    _b("PO%d" % _t, 192, "bfloat16")
    _b("HW%d" % _t, 48, "float32")
for _n, _c in (("Z0", 512), ("Z1", 512), ("Z2", 512), ("CN", 512), ("SS", 512), ("XB", 512), ("Y0", 512), ("Y1", 512)):
    _b(_n, _c, "float32", "psum")

SEMAPHORES = ["qV", "qS", "qT", "qG", "ls"] + ["dm%d" % i for i in range(24)] + ["r%s%d" % (a, t) for a in "eph" for t in range(1, NS)] + ["rf", "ro1"]


def rank_program(g, core, T, topo):
    rank = T.rank_of(core)
    if rank is None:
        return
    cores = T.cores
    n = len(cores)
    eng = {"V": g.vector, "S": g.scalar, "T": g.tensor, "G": g, "Y": g.sync}
    cnt = {"V": 0, "S": 0, "T": 0, "G": 0}
    log = {}
    known = {q: {} for q in "VSTGY"}
    clock = {}
    ndma = [0]
    psum = ("Z0", "Z1", "Z2", "CN", "SS", "XB", "Y0", "Y1")

    def B(name, lo=0, hi=None, step=1, parts=None):
        t = T[name]
        if hi is None:
            hi = SCRATCH[name][1][1]
        if parts is None:
            ap = t[:, lo:hi] if step == 1 else t[:, lo:hi:step]
        else:
            ap = t[parts[0]:parts[1]:parts[2], lo:hi]
        return (ap, [(name, lo, hi)], [])

    def IND(win, off):
        return (win[0].indirect(off[0]), win[1], off[1])

    def ext(ap):
        return (ap, [], [])

    def need(q, reads, writes, acc):
        want = {}
        for regs, wr in ((reads, False), (writes, True)):
            for nm, lo, hi in regs:
                if nm in psum:
                    lo, hi = 0, 512
                for e in log.get(nm, []):
                    if e[0] < hi and lo < e[1] and (wr or e[3]):
                        if e[4] == q and (not e[3] or acc):
                            continue
                        s, v = e[2]
                        if want.get(s, 0) < v:
                            want[s] = v
        for s in sorted(want):
            v = want[s]
            if known[q].get(s, 0) >= v:
                continue
            eng[q].wait_ge(T.sem[s], v)
            for k, w in clock.get((s, v), {}).items():
                if known[q].get(k, 0) < w:
                    known[q][k] = w
            known[q][s] = max(known[q].get(s, 0), v)

    def note(q, tok, reads, writes):
        clock[tok] = dict(known[q])
        for regs, wr in ((reads, False), (writes, True)):
            for nm, lo, hi in regs:
                if nm in psum:
                    lo, hi = 0, 512
                lst = log.get(nm, [])
                if wr:
                    lst = [e for e in lst if not (lo <= e[0] and e[1] <= hi)]
                else:
                    lst = [e for e in lst if not (e[4] == q and not e[3] and lo <= e[0] and e[1] <= hi)]
                lst.append([lo, hi, tok, wr, q])
                log[nm] = lst

    def op(q, fn, out, ins, acc=False, done=True):
        reads = list(out[2])
        for i in ins:
            reads += i[1] + i[2]
        need(q, reads, out[1], acc)
        inst = fn()
        s = "q" + q
        if done:
            cnt[q] += 1
            inst.then_inc(T.sem[s], 1)
            note(q, (s, cnt[q]), reads, out[1])
        else:
            note(q, (s, cnt[q] + 1), reads, out[1])

    def dma(q, out, in_):
        need(q, in_[1], out[1], False)
        s = "dm%d" % ndma[0]
        ndma[0] += 1
        eng[q].dma_start(out[0], in_[0]).then_inc(T.sem[s], 16)
        known[s] = dict(known[q])
        note(s, (s, 16), in_[1], out[1])

    sent = [0]

    def send(dst, out, in_, sem, ne):
        need("G", in_[1], [], False)
        rid, pid, _ = topo.addr(dst)
        es = topo.engines(core, dst)[:ne]
        g.remote_dma(out[0], in_[0], T.sem[sem], T.sem["ls"], pid, rid, sum(1 << e for e in es))
        sent[0] += len(es)

    def arrive(name, lo, hi, src, sem, ne):
        v = len(topo.engines(src, core)[:ne])
        known[sem] = {}
        note(sem, (sem, v), [], [(name, lo, hi)])

    def val(x):
        return x[0] if isinstance(x, tuple) else x

    def opnds(*xs):
        return [x for x in xs if isinstance(x, tuple)]

    def tcopy(out, in_):
        op("V", lambda: g.vector.tensor_copy(out[0], in_[0]), out, [in_])

    def tt(out, a, b, o):
        op("V", lambda: g.vector.tensor_tensor(out[0], a[0], b[0], o), out, [a, b])

    def ts(out, a, s1, o1, s2=None, o2=None):
        if o2 is None:
            op("V", lambda: g.vector.tensor_scalar(out[0], a[0], val(s1), None, o1), out, [a] + opnds(s1))
        else:
            op("V", lambda: g.vector.tensor_scalar(out[0], a[0], val(s1), val(s2), o1, o2), out, [a] + opnds(s1, s2))

    def scan(out, a, b, o1, o2):
        op("V", lambda: g.vector.tensor_tensor_scan(out[0], a[0], b[0], 0.0, o1, o2), out, [a, b])

    def fill(out, c):
        op("V", lambda: g.vector.memset(out[0], c), out, [])

    def act(out, in_, f, bias=0.0, scale=1.0):
        op("S", lambda: g.scalar.activation(out[0], in_[0], f, bias=val(bias), scale=val(scale)), out, [in_] + opnds(bias, scale))

    def mm(out, l, r, st, sp):
        op("T", lambda: g.tensor.matmul(out[0], l[0], r[0], st, sp), out, [l, r], acc=not st, done=sp)

    def iota(out, pat, base, cm):
        op("G", lambda: g.iota(out[0], pat, base, cm, allow_small_or_imprecise_dtypes=True), out, [])

    def col(i):
        return B("cols", i, i + 1)

    H = V // 2
    dma("Y", B("own_s"), ext(T.own[:]))
    dma("Y", B("ki"), ext(T.kin[:]))
    dma("Y", B("PR0", 0, P), ext(T.price[:]))
    dma("Y", B("Xw", 0, V), ext(T.x[:]))
    dma("Y", B("hold_s"), ext(T.hold[:]))
    dma("Y", B("wall_s"), ext(T.wall[:]))
    dma("Y", B("wt_s"), ext(T.wt[:]))

    iota(B("cols", 9, 10), [[0, 1]], 0, 1)
    iota(B("dm0"), [[16, 12]], V, 1)
    iota(B("grow"), [[1, 8], [0, 16]], 0, 0)
    iota(B("irow"), [[0, 8], [1, 16]], 0, 0)
    iota(B("K4"), [[4096, 16], [0, 12]], -65536, 0)
    iota(B("mrow"), [[1, 128]], 0, 0)
    iota(B("jlrow"), [[0, 12], [1, 16]], 0, 0)
    iota(B("lv"), [[1, 8], [16, 16]], 0, 0)
    iota(B("colj"), [[16, 16]], 0, 0)
    RB = 1328
    iota(B("ramp", 0, RB), [[1, RB]], 0, 0)
    act(B("ramp", RB, 2 * RB), B("ramp", 0, RB), F.Identity, bias=float(RB))
    act(B("ramp", 2 * RB, 4 * RB), B("ramp", 0, 2 * RB), F.Identity, bias=float(2 * RB))
    ci = lambda i: B("ci", i, i + 1)
    fill(B("cb"), 0.0)
    fill(B("zero"), 0.0)
    fill(B("ZB"), -128.0)
    tcopy(ci(0), col(9))
    ts(ci(1), ci(0), 4, A.logical_shift_right)
    ts(ci(2), ci(0), 1, A.bitwise_and)
    ts(ci(3), ci(0), 4, A.logical_shift_right, 1, A.bitwise_and)
    ts(ci(0), ci(0), 15, A.bitwise_and)
    tcopy(B("cols", 0, 3), B("ci", 0, 3))
    tcopy(col(6), ci(3))
    ts(col(3), col(2), -1.0, A.mult, 1.0, A.add)
    ts(col(4), col(1), -16.0, A.mult)
    ts(col(5), col(0), 1.0, A.add)
    ts(B("DUM", 0, 12), B("dm0"), col(4), A.add)
    ts(B("DUM", 12, 24), B("dm0"), col(4), A.add)
    ts(B("m12"), B("DUM", 0, 12), -float(V), A.add)
    ts(B("kI"), B("m12"), 1.0 / 12.0, A.mult, -11.0 / 24.0, A.add)
    ts(B("eh"), B("kI"), -12.0, A.mult)
    tt(B("eh"), B("eh"), B("m12"), A.add)
    ts(B("jI"), B("eh"), col(6), A.add)
    ts(B("jI"), B("jI"), 1, A.bitwise_and)
    ts(B("bx"), B("jI"), 208.0, A.mult)
    ts(B("bk"), B("eh"), 16.0, A.mult)
    tt(B("bk"), B("bk"), B("kI"), A.add)
    tt(B("bk"), B("bk"), B("bx"), A.add)
    tcopy(B("SELu"), B("bk"))
    ts(B("BO"), B("grow"), col(1), A.is_equal, 8192.0, A.mult)
    ts(B("gt"), B("irow"), col(0), A.is_gt)
    tt(B("U"), B("BO"), B("gt"), A.mult)
    ts(B("KC"), B("K4"), 1.0 / 131072.0, A.mult)
    fill(B("KZ"), -2176.0)
    for a, b in CH[1:]:
        o = 24 * (a - C0)
        tcopy(B("KZ", o, o + 12 * (b - a)), B("KC", 12 * a, 12 * b))
    tcopy(B("XB", 192, 384), B("K4"))
    ts(B("IDF"), B("mrow"), col(9), A.is_equal)
    ts(B("ID"), B("mrow"), col(9), A.is_equal)
    ts(B("NID"), B("ID"), -1.0, A.mult)
    ts(B("c3t"), B("jlrow"), col(0), A.is_lt, -LOW, A.mult)
    ts(B("C3"), B("jlrow"), col(0), A.is_equal, BIG, A.mult)
    tt(B("C3"), B("C3"), B("c3t"), A.add)
    ts(col(8), col(0), 0.0, A.is_equal, -LOW, A.mult)
    ts(B("c3t"), B("jlrow"), 15.0, A.is_equal, col(8), A.mult)
    tt(B("C3"), B("C3"), B("c3t"), A.add)
    ts(col(11), col(8), -1.0, A.mult, -BIG, A.add)
    ts(B("colj"), B("colj"), col(1), A.add)
    for j in range(16):
        ts(B("LA", 128 * j, 128 * j + 128), B("lv"), B("colj", j, j + 1), A.is_equal, 65536.0, A.mult)
    ts(B("LB"), B("LA"), 512.0, A.mult)
    ts(B("WKB"), B("grow"), col(1), A.is_equal, col(5), A.mult)
    tcopy(B("E0"), B("own_s"))

    DIAG = (T.eq[:, :, 0:16], [("eq", 0, 192)], [])
    nxt = cores[(rank + 1) % n]
    prv = cores[(rank - 1) % n]
    NE, NP = 16, 16
    late = []

    def absd(a, b, sign=False):
        if a < C0:
            return B("aa", a * P, b * P)
        ca, cb = [c for c in CH if c[0] <= a < c[1]][0]
        o = 2 * (ca - C0) + (a - ca) + (cb - ca if sign else 0)
        return B("as", o * P, (o + b - a) * P)

    def sums(i):
        y = "Y%d" % (i % 2)
        mm(B(y, 0, 512), B("WKB"), B("Kw", 512 * i, 512 * i + 512), True, True)

    def sums_out(i):
        y = "Y%d" % (i % 2)
        act(B("Yw", 512 * i, 512 * i + 512), B(y, 0, 512), F.Copy)

    for t in range(NS):
        jub = t % 2 == 1
        EU, PR, HW, OF = "E%d" % t, "PR%d" % t, "HW%d" % t, "of%d" % (t % 2)
        OX, OK = B(OF, 0, 12), B(OF, 12, 24)
        EO, PO, HN = "EO%d" % t, "PO%d" % t, "HW%d" % (t + 1)
        if t:
            arrive(EU, 0, 12, prv, "re%d" % t, NE)
            arrive(PR, 0, P, prv, "rp%d" % t, NP)
            arrive(HW, 0, 36 if t == 3 else 24, prv, "rh%d" % t, NE)
            if t == 1:
                arrive(HW, 24, 36, prv, "ro1", NE)
        tcopy(B("cb", 16, 208), IND(B("Kw" if t else "ki", 0, V), B(EU)))
        op("V", lambda: g.vector.transpose(T.tr[:, 0:192], T.cb[:, 16:208]), B("tr", 0, 192), [B("cb", 16, 208)])
        op("V", lambda: g.vector.transpose(T.tr[:, 192:416], T.cb[:, 0:224]), B("tr", 192, 416), [B("cb")])
        tcopy(B("cTu"), IND(B("tr"), B("SELu")))
        act(B("cTf"), IND(B("tr"), B("SELu")), F.Copy)
        if t == 0:
            tcopy(B("Kw", 0, H), B("ki", 0, H))
            late = [lambda: tcopy(B("HW0", 0, 12), B("hold_s")),
                    lambda: tcopy(B("HW0", 12, 24), B("wall_s")),
                    lambda: send(nxt, B("HW1", 0, 24), B("HW0", 0, 24), "rh1", NE),
                    lambda: tcopy(col(7), B("wt_s")),
                    lambda: ts(B("BW"), B("grow"), col(1), A.is_equal, col(7), A.mult)]
        if t == 2:
            late.pop(0)()
            sums(0)
            sums(1)
        if t == 1:
            mm(B("SS", 0, 16), B("BW"), B("ZB", 0, 16), True, True)
            late = [lambda: ts(col(12), B("SS", 0, 1), 130.0 / 128.0, A.mult, col(11), A.add)]
        act(B(PR, 192, 384), B(PR, 0, 192), F.Copy)
        act(B(PR, 384, 768), B(PR, 0, 384), F.Copy)
        side = []

        def fillers():
            if side:
                side.pop(0)()
        for a, b, ab, sn, iv in SG:
            tt(B("d", a * P, b * P), IND(B("Xw", 0, V), B("cTu", 12 * a, 12 * b)), B(PR, 0, (b - a) * P), A.subtract)
            if a == 0:
                tt(B("K4c"), B("XB", 192, 384), B("cTf"), A.add)
            if ab is not None:
                act(absd(ab, b), B("d", ab * P, b * P), F.Abs)
            if sn is not None:
                act(B("sg", sn * P, b * P), B("d", sn * P, b * P), F.Sign, bias=-0.5, scale=-1.0)
            if iv is not None and iv < C0:
                ts(B("sg", iv * P, b * P), B("d", iv * P, b * P), 0.0, A.is_lt, -0.5, A.add)
            elif iv is not None:
                ts(absd(iv, b, True), B("d", iv * P, b * P), 0.0, A.is_lt, 512.0, A.mult)
        act(B("q"), B(PR, 0, P), F.Identity, bias=129.625, scale=0.25)
        if t == 0:
            act(B("Hw", 0, V), B("ramp", 0, V), F.Copy)
        for c, (a, b) in enumerate(CH):
            z = ("Z0", "Z1", "Z2", "CN")[c]
            w = 12 * (b - a)
            zb = w if c else 128
            if c == 0:
                mm(B(z, 0, w), B("BO"), B("KC", 0, w), True, False)
                mm(B(z, 0, w), B("IDF"), B("cTf", 0, w), False, False)
                for j in range(16):
                    mm(B(z, 0, w), B("LA", 128 * j, 128 * j + 128), B("aa", j, b * P, 16), False, j == 15)
                mm(B(z, 128, 128 + w), B("BO"), B("ZB", 0, w), True, False)
                for j in range(16):
                    mm(B(z, 128, 128 + w), B("LB", 128 * j, 128 * j + 128), B("sg", j, b * P, 16), False, j == 15)
            else:
                lo, hi = 2 * (a - C0), 2 * (b - C0)
                mm(B(z, 0, 2 * w), B("BO"), B("KZ", 12 * lo, 12 * hi), True, False)
                mm(B(z, 0, w), B("IDF"), B("cTf", 12 * a, 12 * b), False, False)
                for j in range(16):
                    mm(B(z, 0, 2 * w), B("LA", 128 * j, 128 * j + 128), B("as", lo * P + j, hi * P, 16), False, j == 15)
            if c == 0:
                side = [lambda: ts(B("eF"), B(EU), float(FB), A.add),
                        lambda: ts(B("eB"), B(EU), col(11), A.add)]
                if t == 0:
                    side = [lambda: tcopy(B("Kw", H, V), B("ki", H, V))] + side
                if jub:
                    side += [lambda: ts(B("wF"), B(HW, 24, 36), float(V), A.is_lt),
                             lambda: tt(B("th"), B(HW, 24, 36), B(HW, 0, 12), A.subtract),
                             lambda: ts(B("nw"), B(HW, 12, 24), -1.0, A.mult, 1.0, A.add),
                             lambda: tt(B("th"), B("th"), B("wF"), A.mult),
                             lambda: ts(B("Aw"), B("nw"), col(11), A.mult),
                             lambda: tt(B(HW, 0, 12), B("th"), B(HW, 0, 12), A.add),
                             lambda: tt(B("hW"), B(HW, 0, 12), B(HW, 12, 24), A.mult),
                             lambda: tt(B("hW"), B("hW"), B("Aw"), A.add)]
                side += late
                late = []
            if c == 3:
                while side:
                    fillers()
                if t == 2:
                    sums_out(0)
                    sums_out(1)
                    sums(2)
            tt(B("t1", 12 * a, 12 * b), B(z, zb, zb + w), B("K4c", 12 * a, 12 * b), A.max)
            if c == 3:
                tt(B("t1", 180, 192), B("t1", 180, 192), B("keys", 168, 180), A.min)
                tt(B("KEY"), B(z, 0, w), B("t1", 180, 192), A.min)
                break
            fillers()
            if c == 2:
                tt(B("t1", 144, 180), B("t1", 144, 180), B("keys", 0, 36), A.min)
                fillers()
            tt(B("keys", 12 * a, 12 * b), B(z, 0, w), B("t1", 12 * a, 12 * b), A.min)
            fillers()
            if c == 1:
                tt(B("keys", 0, 72), B("keys", 0, 72), B("keys", 72, 144), A.min)
                fillers()
                tt(B("keys", 0, 36), B("keys", 0, 36), B("keys", 36, 72), A.min)
                fillers()
            if c == 2:
                tt(B("keys", 144, 156), B("keys", 144, 156), B("keys", 156, 168), A.min)
                fillers()
                tt(B("keys", 168, 180), B("keys", 144, 156), B("keys", 168, 180), A.min)
        ts(B("bI"), B("KEY"), 4095, A.bitwise_and)
        tt(B("fe"), B("KEY"), B("eF"), A.min)
        tcopy(B("bU"), B("bI"))
        tt(B("dk"), B("fe"), B("bI"), A.max)
        ts(B("ek"), B("KEY"), 0.0, A.is_lt, 8192.0, A.mult)
        tcopy(B("dkU"), B("dk"))
        ts(B("dkB"), B("dk"), col(11), A.add)
        tcopy(B("dkf"), IND(B("ramp"), B("dkU")))
        act(B("bF"), IND(B("ramp", 0, V), B("bU")), F.Copy)
        act(B("Xb"), IND(B("Xw", 0, V), B("bU")), F.Copy)
        act(B("Fo"), IND(B("Kw", 0, V), B("bU")), F.Identity, scale=col(2))
        act(B("ce"), B("cb", 16, 208), F.Identity, scale=col(3))
        mm(B("CN", 0, P), B("BO"), B("zero"), True, False)
        for j in range(12):
            w = P - 16 * j
            op("V", lambda: g.vector.tensor_scalar(T.eq[:, j, 0:w], T.dkf[:, 16 * j:P], T.dk[:, j:j + 1], None, A.is_equal),
               (None, [("eq", 16 * j, 16 * j + 16)], []), [B("dkf"), B("dk")])
            if j < 11:
                mm(B("CN", 16 * j + 16, P), B("BO"), (T.eq[:, j, 16:w], [("eq", 16 * j, 16 * j + 16)], []), False, False)
        mm(B("CN", 0, P), B("U"), DIAG, False, True)
        mm(B("XB", 0, P), B("ID"), B("Xb"), True, False)
        mm(B("XB", 0, P), B("NID"), B("q"), False, True)
        if t == 2:
            sums_out(2)
            sums(3)
            sums(4)
        act(B("xr"), B("XB", 0, P), F.Relu, bias=130.0)
        tt(B("ek"), B("ek"), B("eB"), A.add)
        if jub:
            tt(B("th"), B("bI"), B(HW, 0, 12), A.subtract)
        scan(B("sc3"), B("CN", 0, P), B("C3"), A.max, A.add)
        oX = B(HW, 24, 36)
        tt(B("bxk", 12, 24), B("sc3", 15, P, 16), B("ek"), A.add)
        tt(B("bxk", 0, 12), B("sc3", 15, P, 16), B("dkB"), A.add)
        if jub:
            tt(B("th"), B("th"), B(HW, 12, 24), A.mult)
        tt(B(HW, 24, 48), B("bxk"), B("DUM"), A.min)
        tcopy(B(OF), B(HW, 24, 48))
        ts(B("wU"), oX, float(V), A.is_lt)
        tcopy(IND(B("Hw"), OK), B("bF"))
        act(B("hm"), IND(B("Hw", 0, V), B(EU)), F.Copy)
        if t == NS - 1:
            dma("Y", ext(T.yh[:]), B("Hw", 0, V, parts=(0, 128, 16)))
        if t == 2:
            sums_out(3)
            sums_out(4)
        if t == NS - 1:
            tcopy(IND(B("Xw"), OX), B("xr"))
            dma("Y", ext(T.yx[:]), B("Xw", 0, V))
        if jub:
            act(B("wb"), IND(B("ramp", 0, 16), B("wU")), F.Copy)
            mm(B("Z2", 0, P), B("ID"), B("wb"), True, False)
            mm(B("Z2", 0, P), B("ID"), B(PR, 0, P), False, True)
            act(B("pj"), B("Z2", 0, P), F.Relu, bias=15.0, scale=-1.0)
            act(B("pw"), B("pj"), F.Identity, bias=15.0, scale=-1.0)
            ts(B("wF"), oX, float(V), A.is_lt)
            tt(B("th"), B("th"), B("wF"), A.mult)
            tt(B("Aw"), B("th"), B("hW"), A.add)
        else:
            tt(B("pj"), IND(B("ramp", 0, 16), B("wU")), B(PR, 0, P), A.add)
        if t >= 2:
            yv = "yv%d" % t
            mm(B("Y1", 0, P), B("WKB"), B("Fo"), True, False)
            mm(B("Y1", 0, P), B("WKB"), B("ce"), False, True)
            act(B(yv), B("Y1", 0, P), F.Copy)
        scan(B("sc"), B("hm"), B("C3"), A.max, A.add)
        el = B("sc", 15, 192, 16)
        if jub:
            tt(B("eh"), el, B("nw"), A.mult)
            tt(B("fin", 0, 12), B("eh"), B("Aw"), A.add)
            tcopy(B(EO), B("fin", 0, 12))
        else:
            ts(B(EO), el, col(11), A.add)
        if t < NS - 1:
            send(nxt, B("E%d" % (t + 1)), B(EO), "re%d" % (t + 1), NE)
        if not jub:
            ts(B(PO), B("pj"), 15.0, A.min)
            send(nxt, B("PR%d" % (t + 1), 0, P), B(PO), "rp%d" % (t + 1), NP)
            if t == 0:
                send(nxt, B(HN, 24, 36), B(HW, 24, 36), "ro1", NE)
            else:
                send(nxt, B(HN, 0, 36), B(HW, 0, 36), "rh%d" % (t + 1), NE)
            tt(IND(B("Kw"), OK), B("Fo"), B("ce"), A.add)
        if t < NS - 1:
            tcopy(IND(B("Xw"), OX), B("xr"))
        if jub:
            tt(B("pj"), IND(B("Xw", 0, V), B(EO)), B("pw"), A.add)
            ts(B("ph"), B("pj"), 0.5, A.mult, 129.75, A.add)
            mm(B("SS", 0, P), B("BW"), B("ph"), True, True)
            if t < NS - 1:
                ts(B(PO), B("ph"), -130.0, A.add)
                send(nxt, B("PR%d" % (t + 1), 0, P), B(PO), "rp%d" % (t + 1), NP)
                tt(IND(B("Kw"), OK), B("Fo"), B("ce"), A.add)

            def holders(t=t, HW=HW, HN=HN):
                def home():
                    if t < NS - 1:
                        tt(B(HW, 0, 12), B("uI"), B("gg"), A.add)
                        send(nxt, B(HN, 0, 24), B(HW, 0, 24), "rh%d" % (t + 1), NE)
                    else:
                        tt(B("fin", 12, 24), B("uI"), B("gg"), A.add)
                        send(cores[(rank - t) % n], B("rfin"), B("fin"), "rf", NE)
                return [lambda: scan(B("sc3"), B("SS", 0, P), B("C3"), A.max, A.add),
                        lambda: ts(B("sI"), B("sc3", 15, P, 16), col(12), A.add),
                        lambda: ts(B("uI"), B("sI"), 4095, A.bitwise_and),
                        lambda: ts(B("gg"), B("uI"), float(V), A.is_ge, -float(V), A.mult),
                        home]
            if t == NS - 1:
                for f in holders():
                    f()
            else:
                late = holders()
    tcopy(IND(B("Yw"), B("of0", 12, 24)), B("yv2"))
    tcopy(IND(B("Yw"), B("of1", 12, 24)), B("yv3"))
    dma("Y", ext(T.yk[:]), B("Yw", 0, V, parts=(0, 128, 16)))
    arrive("rfin", 0, 24, cores[(rank + NS - 1) % n], "rf", NE)
    tcopy(B("rU"), B("rfin"))
    tcopy(B("outf", 0, P), IND(B("ramp", 0, V), B("rU", 0, 12)))
    act(B("outf", P, 2 * P), IND(B("ramp", 0, V), B("rU", 12, 24)), F.Copy)
    dma("Y", ext(T.yo[:]), B("outf", 0, P, parts=(0, 128, 16)))
    dma("S", ext(T.yt[:]), B("outf", P, 2 * P, parts=(0, 128, 16)))
    g.wait_ge(T.sem["ls"], sent[0])
    for i in range(ndma[0]):
        g.wait_ge(T.sem["dm%d" % i], 16)
    for q in "VST":
        g.wait_ge(T.sem["q" + q], cnt[q])
    g.wait_ge(T.sem["qG"], cnt["G"])
